import numpy as np
import ml_dtypes


def mxq(x, axis, fmt="e4m3"):
    dtype, down = {"e4m3": (ml_dtypes.float8_e4m3fn, 7), "e5m2": (ml_dtypes.float8_e5m2, 14)}[fmt]
    v = np.moveaxis(np.asarray(x, np.float32).astype(ml_dtypes.bfloat16).astype(np.float64), axis, -1)
    blocks = v.reshape(v.shape[:-1] + (-1, 32))
    amax = np.abs(blocks).max(-1, keepdims=True)
    byte = np.maximum(np.where(amax > 0, np.frexp(amax)[1] - 1 + 127, 0) - down, 1)
    scale = np.exp2(byte - 127.0)
    codes = (blocks / scale).astype(np.float32).astype(dtype).astype(np.float64)
    return np.moveaxis((codes * scale).reshape(v.shape), -1, axis)


WIDE = False


def mx_kscale(k):
    if not WIDE:
        return np.ones(k)
    levels = np.array([10, -10, 5, -5, 0])
    if k % 512:
        return np.exp2(np.random.permutation(np.resize(levels, k // 32))).repeat(32)
    a = np.empty((k // 512, 16))
    for p in range(k // 512):
        a[p, :8] = np.random.permutation(np.resize(levels, 8))
        for g in range(8):
            far = levels[np.abs(levels - a[p, g]) >= 10]
            a[p, g + 8] = far[np.random.randint(len(far))]
    return np.exp2(a.ravel()).repeat(32)


def f64(x):
    return np.asarray(x).astype(np.float64)


def striped(idx):
    return np.tile(idx.reshape(-1, 16).T, (8, 1)).astype(np.uint16)


def unstriped(offs):
    return offs[:16].T.reshape(-1).astype(np.int64)


def pack_weight(w):
    k, n = w.shape
    w = f64(np.asarray(w, np.float32).astype(ml_dtypes.bfloat16)).reshape(k // 32, 32, n)
    amax = np.abs(w).max(1)
    byte = np.clip(np.where(amax > 0, np.frexp(amax)[1] - 1 + 127 - 7, 1), 1, 254)
    scaled = (w * np.exp2(127.0 - byte)[:, None, :]).reshape(k, n).astype(np.float32)
    words = np.ascontiguousarray(scaled.reshape(k // 512, 128, 4, n).transpose(0, 1, 3, 2)).astype(ml_dtypes.float8_e4m3fn).view(np.uint8)
    return words, np.ascontiguousarray(byte.astype(np.uint8).reshape(k // 512, 16, n))


def unpack_weight(words, scales):
    g, p, n, _ = words.shape
    vals = np.ascontiguousarray(words).view(ml_dtypes.float8_e4m3fn).astype(np.float64) * np.repeat(np.exp2(scales.astype(np.float64) - 127.0), 8, axis=1)[..., None]
    return vals.transpose(0, 1, 3, 2).reshape(g * 512, n)


def sigmoid(v):
    return 1.0 / (1.0 + np.exp(-np.maximum(v, -700.0)))


K, T, S, N, U = 512, 1024, 512, 256, 1024


def setup_inputs():
    n = np.random.standard_normal
    s = mx_kscale(K)[:, None]
    packed_w1 = pack_weight(n((K, N)) / np.sqrt(K) / s)
    packed_w2 = pack_weight(n((K, N)) / np.sqrt(K) / s)
    return {
        "xT": (n((K, T)) * s).astype(np.float32),
        "mem": n((N, U)).astype(np.float32),
        "w1_words": packed_w1[0],
        "w1_scales": packed_w1[1],
        "w2_words": packed_w2[0],
        "w2_scales": packed_w2[1],
        "offs": striped(np.random.permutation(T)[:S]),
        "slot": striped(np.random.permutation(U)[:S]),
    }


def reference(xT, mem, w1_words, w1_scales, w2_words, w2_scales, offs, slot):
    old = f64(mem)[:, unstriped(slot)]
    xq = mxq(f64(xT)[:, unstriped(offs)], 0, "e4m3")
    g = sigmoid(unpack_weight(w2_words, w2_scales).T @ xq)
    y = np.tanh(unpack_weight(w1_words, w1_scales).T @ xq)
    out = f64(mem).copy()
    out[:, unstriped(slot)] = old + g * (y - old)
    return out

@@ -1,0 +1,128 @@
+from contextlib import ExitStack
+
+import concourse.mybir as mybir
+
+K, T, S, N, U = 512, 1024, 512, 256, 1024
+FLOPS = 2 * 2 * K * N * S
+
+F32 = mybir.dt.float32
+BF16 = mybir.dt.bfloat16
+I32 = mybir.dt.int32
+U32 = mybir.dt.uint32
+U16 = mybir.dt.uint16
+U8 = mybir.dt.uint8
+FP8X4 = mybir.dt.float8_e4m3fn_x4
+ACT = mybir.ActivationFunctionType
+ALU = mybir.AluOpType
+
+P = 128
+PACK = 4
+HALF = S // 2
+LIST_ROWS = 16
+
+
+def tile_picked_gmem_tanh_e_kernel(
+    tc, xT, mem, w1_words, w1_scales, w2_words, w2_scales, offs, slot, out
+):
+    nc = tc.nc
+    with ExitStack() as ctx:
+        keep = ctx.enter_context(tc.tile_pool(name="keep", bufs=1))
+        psum = ctx.enter_context(tc.psum_pool(name="psum", bufs=1))
+
+        offs_sb = keep.tile([P, S // LIST_ROWS], U16, name="offs_sb")
+        slot_sb = keep.tile([P, S // LIST_ROWS], U16, name="slot_sb")
+        x_rows = [keep.tile([P, T], F32, name="x_row%d" % j) for j in range(PACK)]
+        window = [keep.tile([P, U], F32, name="window%d" % b) for b in range(2)]
+        w_codes = [keep.tile([P, N], U32, name="w_codes%d" % i, align_bytes=64) for i in range(2)]
+        w_bytes = [keep.tile([P, N], U8, name="w_bytes%d" % i, align_bytes=64) for i in range(2)]
+
+        def entries(lst, lo, hi):
+            return lst[:, lo // LIST_ROWS : hi // LIST_ROWS]
+
+        for i in range(2):
+            nc.vector.memset(w_bytes[i][:].bitcast(I32), 0)
+        warm = keep.tile([P, 2], F32, name="warm")
+        nc.vector.memset(warm[:, 0:1], 0.0)
+        nc.scalar.activation(warm[:, 1:2], warm[:, 0:1], ACT.Sigmoid)
+
+        x_view = xT.rearrange("(p j) t -> p j t", j=PACK)
+        nc.sync.dma_start(offs_sb[:], offs)
+        for j in range(PACK):
+            nc.sync.dma_start(x_rows[j][:], x_view[:, j, :])
+        for i, scales in enumerate((w1_scales, w2_scales)):
+            for q in range(4):
+                nc.scalar.dma_start(
+                    w_bytes[i][32 * q : 32 * q + 4, :].bitcast(I32), scales[0, 4 * q : 4 * q + 4, :].bitcast(I32)
+                )
+        for i, words in enumerate((w1_words, w2_words)):
+            nc.sync.dma_start(w_codes[i][:].bitcast(I32), words[0].rearrange("p n t -> p (n t)").bitcast(I32))
+        nc.sync.dma_start(slot_sb[:], slot)
+        for b in range(2):
+            nc.sync.dma_start(window[b][:], mem[b * P : (b + 1) * P, :])
+
+        picked = keep.tile([P, PACK, S], BF16, name="picked")
+        for j in range(PACK - 1):
+            nc.vector.tensor_copy(picked[:, j, :], x_rows[j][:].indirect(offs_sb[:]))
+        for h in range(2):
+            lo, hi = h * HALF, (h + 1) * HALF
+            nc.vector.tensor_copy(picked[:, PACK - 1, lo:hi], x_rows[PACK - 1][:].indirect(entries(offs_sb, lo, hi)))
+
+        old = [keep.tile([P, S], F32, name="old%d" % b) for b in range(2)]
+        acc = [[psum.tile([P, HALF], F32, name="acc%d_%d_%d" % (i, b, h)) for h in range(2)] for b in range(2) for i in range(2)]
+        keep_gate = [keep.tile([P, S], F32, name="keep_gate%d" % b) for b in range(2)]
+        neg_cand = [keep.tile([P, S], F32, name="neg_cand%d" % b) for b in range(2)]
+        grouped = [keep.tile([P, HALF, PACK], BF16, name="grouped%d" % h, align_bytes=64) for h in range(2)]
+        x_codes = [keep.tile([P, HALF], U32, name="x_codes%d" % h, align_bytes=64) for h in range(2)]
+        x_bytes = [keep.tile([P, HALF], U8, name="x_bytes%d" % h, align_bytes=64) for h in range(2)]
+        for h in range(2):
+            lo, hi = h * HALF, (h + 1) * HALF
+            nc.scalar.copy(
+                grouped[h][:].rearrange("p (c i) t -> p c t i", i=4),
+                picked[:, :, lo:hi].rearrange("p t (c i) -> p c t i", i=4),
+            )
+        for h in range(2):
+            nc.vector.tensor_copy(old[h][:], window[h][:].indirect(slot_sb[:]))
+            nc.vector.quantize_mx(
+                out=x_codes[h][:].bitcast(FP8X4),
+                scales=x_bytes[h][:],
+                in_=grouped[h][:].rearrange("p c t -> p (c t)"),
+            )
+            for b in range(2):
+                for i in (1, 0):
+                    nc.tensor.matmul_mx(
+                        out=acc[2 * b + i][h][:],
+                        lhsT=w_codes[i][:, b * P : (b + 1) * P].bitcast(FP8X4),
+                        lhsT_scale=w_bytes[i][:, b * P : (b + 1) * P],
+                        rhs=x_codes[h][:].bitcast(FP8X4),
+                        rhs_scale=x_bytes[h][:],
+                        start=True,
+                        stop=True,
+                    )
+        for b in range(2):
+            for h in range(2):
+                lo, hi = h * HALF, (h + 1) * HALF
+                nc.scalar.activation(keep_gate[b][:, lo:hi], acc[2 * b + 1][h][:], ACT.Sigmoid, scale=-1.0)
+                nc.scalar.activation(neg_cand[b][:, lo:hi], acc[2 * b][h][:], ACT.Tanh, scale=-1.0)
+
+        kept = [keep.tile([P, S], F32, name="kept%d" % b) for b in range(2)]
+        added = [keep.tile([P, S], F32, name="added%d" % b) for b in range(2)]
+
+        def blend(b, lo, hi):
+            nc.vector.tensor_tensor(kept[b][:, lo:hi], old[b][:, lo:hi], keep_gate[b][:, lo:hi], ALU.mult)
+            nc.vector.scalar_tensor_tensor(
+                added[b][:, lo:hi], keep_gate[b][:, lo:hi], 1.0, neg_cand[b][:, lo:hi], ALU.subtract, ALU.mult
+            )
+
+        def put(b, lo, hi):
+            nc.vector.tensor_tensor(
+                window[b][:].indirect(entries(slot_sb, lo, hi)), kept[b][:, lo:hi], added[b][:, lo:hi], ALU.add
+            )
+
+        blend(0, 0, HALF)
+        put(0, 0, HALF)
+        blend(0, HALF, S)
+        blend(1, 0, S)
+        put(0, HALF, S)
+        nc.sync.dma_start(out[0:P, :], window[0][:])
+        put(1, 0, S)
+        nc.sync.dma_start(out[P : 2 * P, :], window[1][:])

@@ -41,9 +41,6 @@ def tile_picked_gmem_tanh_e_kernel(
 
         for i in range(2):
             nc.vector.memset(w_bytes[i][:].bitcast(I32), 0)
-        warm = keep.tile([P, 2], F32, name="warm")
-        nc.vector.memset(warm[:, 0:1], 0.0)
-        nc.scalar.activation(warm[:, 1:2], warm[:, 0:1], ACT.Sigmoid)
 
         x_view = xT.rearrange("(p j) t -> p j t", j=PACK)
         nc.sync.dma_start(offs_sb[:], offs)

@@ -17,8 +17,9 @@ ALU = mybir.AluOpType
 
 P = 128
 PACK = 4
-HALF = S // 2
 LIST_ROWS = 16
+PIECES = ((0, 128), (128, 256), (256, 512))
+CAND, GATE = 0, 1
 
 
 def tile_picked_gmem_tanh_e_kernel(
@@ -35,77 +36,82 @@ def tile_picked_gmem_tanh_e_kernel(
         window = [keep.tile([P, U], F32, name="window%d" % b) for b in range(2)]
         w_codes = [keep.tile([P, N], U32, name="w_codes%d" % i, align_bytes=64) for i in range(2)]
         w_bytes = [keep.tile([P, N], U8, name="w_bytes%d" % i, align_bytes=64) for i in range(2)]
+        warm = keep.tile([P, 2], F32, name="warm")
 
         def entries(lst, lo, hi):
             return lst[:, lo // LIST_ROWS : hi // LIST_ROWS]
 
-        for i in range(2):
+        for i in (GATE, CAND):
             nc.vector.memset(w_bytes[i][:].bitcast(I32), 0)
+        nc.vector.memset(warm[:, 0:1], 0.0)
 
         x_view = xT.rearrange("(p j) t -> p j t", j=PACK)
+        nc.sync.dma_start(x_rows[0][:], x_view[:, 0, :])
         nc.sync.dma_start(offs_sb[:], offs)
-        for j in range(PACK):
+        for j in range(1, PACK - 1):
             nc.sync.dma_start(x_rows[j][:], x_view[:, j, :])
-        for i, scales in enumerate((w1_scales, w2_scales)):
+        nc.sync.dma_start(slot_sb[:], slot)
+        nc.sync.dma_start(x_rows[PACK - 1][:], x_view[:, PACK - 1, :])
+        for i, words in ((GATE, w2_words), (CAND, w1_words)):
+            nc.sync.dma_start(w_codes[i][:].bitcast(I32), words[0].rearrange("p n t -> p (n t)").bitcast(I32))
+        nc.sync.dma_start(window[0][:], mem[0:P, :])
+        nc.sync.dma_start(window[1][:], mem[P : 2 * P, :])
+        for i, scales in ((GATE, w2_scales), (CAND, w1_scales)):
             for q in range(4):
                 nc.scalar.dma_start(
                     w_bytes[i][32 * q : 32 * q + 4, :].bitcast(I32), scales[0, 4 * q : 4 * q + 4, :].bitcast(I32)
                 )
-        for i, words in enumerate((w1_words, w2_words)):
-            nc.sync.dma_start(w_codes[i][:].bitcast(I32), words[0].rearrange("p n t -> p (n t)").bitcast(I32))
-        nc.sync.dma_start(slot_sb[:], slot)
-        for b in range(2):
-            nc.sync.dma_start(window[b][:], mem[b * P : (b + 1) * P, :])
+        nc.scalar.activation(warm[:, 1:2], warm[:, 0:1], ACT.Sigmoid)
 
         picked = keep.tile([P, PACK, S], BF16, name="picked")
         for j in range(PACK - 1):
             nc.vector.tensor_copy(picked[:, j, :], x_rows[j][:].indirect(offs_sb[:]))
-        for h in range(2):
-            lo, hi = h * HALF, (h + 1) * HALF
+        for lo, hi in PIECES:
             nc.vector.tensor_copy(picked[:, PACK - 1, lo:hi], x_rows[PACK - 1][:].indirect(entries(offs_sb, lo, hi)))
 
-        old = [keep.tile([P, S], F32, name="old%d" % b) for b in range(2)]
-        acc = [[psum.tile([P, HALF], F32, name="acc%d_%d_%d" % (i, b, h)) for h in range(2)] for b in range(2) for i in range(2)]
+        grouped = {lo: keep.tile([P, hi - lo, PACK], BF16, name="grouped%d" % lo, align_bytes=64) for lo, hi in PIECES}
+        x_codes = {lo: keep.tile([P, hi - lo], U32, name="x_codes%d" % lo, align_bytes=64) for lo, hi in PIECES}
+        x_bytes = {lo: keep.tile([P, hi - lo], U8, name="x_bytes%d" % lo, align_bytes=64) for lo, hi in PIECES}
+        old = keep.tile([P, S], F32, name="old")
         keep_gate = [keep.tile([P, S], F32, name="keep_gate%d" % b) for b in range(2)]
         neg_cand = [keep.tile([P, S], F32, name="neg_cand%d" % b) for b in range(2)]
-        grouped = [keep.tile([P, HALF, PACK], BF16, name="grouped%d" % h, align_bytes=64) for h in range(2)]
-        x_codes = [keep.tile([P, HALF], U32, name="x_codes%d" % h, align_bytes=64) for h in range(2)]
-        x_bytes = [keep.tile([P, HALF], U8, name="x_bytes%d" % h, align_bytes=64) for h in range(2)]
-        for h in range(2):
-            lo, hi = h * HALF, (h + 1) * HALF
-            nc.scalar.copy(
-                grouped[h][:].rearrange("p (c i) t -> p c t i", i=4),
-                picked[:, :, lo:hi].rearrange("p t (c i) -> p c t i", i=4),
-            )
-        for h in range(2):
-            nc.vector.tensor_copy(old[h][:], window[h][:].indirect(slot_sb[:]))
-            nc.vector.quantize_mx(
-                out=x_codes[h][:].bitcast(FP8X4),
-                scales=x_bytes[h][:],
-                in_=grouped[h][:].rearrange("p c t -> p (c t)"),
-            )
-            for b in range(2):
-                for i in (1, 0):
-                    nc.tensor.matmul_mx(
-                        out=acc[2 * b + i][h][:],
-                        lhsT=w_codes[i][:, b * P : (b + 1) * P].bitcast(FP8X4),
-                        lhsT_scale=w_bytes[i][:, b * P : (b + 1) * P],
-                        rhs=x_codes[h][:].bitcast(FP8X4),
-                        rhs_scale=x_bytes[h][:],
-                        start=True,
-                        stop=True,
-                    )
-        for b in range(2):
-            for h in range(2):
-                lo, hi = h * HALF, (h + 1) * HALF
-                nc.scalar.activation(keep_gate[b][:, lo:hi], acc[2 * b + 1][h][:], ACT.Sigmoid, scale=-1.0)
-                nc.scalar.activation(neg_cand[b][:, lo:hi], acc[2 * b][h][:], ACT.Tanh, scale=-1.0)
-
         kept = [keep.tile([P, S], F32, name="kept%d" % b) for b in range(2)]
         added = [keep.tile([P, S], F32, name="added%d" % b) for b in range(2)]
 
-        def blend(b, lo, hi):
-            nc.vector.tensor_tensor(kept[b][:, lo:hi], old[b][:, lo:hi], keep_gate[b][:, lo:hi], ALU.mult)
+        def interleave(lo, hi):
+            nc.scalar.copy(
+                grouped[lo][:].rearrange("p (c i) t -> p c t i", i=4),
+                picked[:, :, lo:hi].rearrange("p t (c i) -> p c t i", i=4),
+            )
+
+        def quantise(lo, hi):
+            nc.vector.quantize_mx(
+                out=x_codes[lo][:].bitcast(FP8X4),
+                scales=x_bytes[lo][:],
+                in_=grouped[lo][:].rearrange("p c t -> p (c t)"),
+            )
+
+        def gates(b, pieces):
+            first, last = pieces[0][0], pieces[-1][1]
+            acc = [psum.tile([P, last - first], F32, name="acc%d_%d_%d" % (i, b, first)) for i in range(2)]
+            for i in (GATE, CAND):
+                for lo, hi in pieces:
+                    nc.tensor.matmul_mx(
+                        out=acc[i][:, lo - first : hi - first],
+                        lhsT=w_codes[i][:, b * P : (b + 1) * P].bitcast(FP8X4),
+                        lhsT_scale=w_bytes[i][:, b * P : (b + 1) * P],
+                        rhs=x_codes[lo][:].bitcast(FP8X4),
+                        rhs_scale=x_bytes[lo][:],
+                        start=True,
+                        stop=True,
+                    )
+            nc.scalar.activation(keep_gate[b][:, first:last], acc[GATE][:], ACT.Sigmoid, scale=-1.0)
+            nc.scalar.activation(neg_cand[b][:, first:last], acc[CAND][:], ACT.Tanh, scale=-1.0)
+
+        def keep_part(lo, hi):
+            nc.vector.tensor_tensor(kept[0][:, lo:hi], old[:, lo:hi], keep_gate[0][:, lo:hi], ALU.mult)
+
+        def add_part(b, lo, hi):
             nc.vector.scalar_tensor_tensor(
                 added[b][:, lo:hi], keep_gate[b][:, lo:hi], 1.0, neg_cand[b][:, lo:hi], ALU.subtract, ALU.mult
             )
@@ -115,11 +121,29 @@ def tile_picked_gmem_tanh_e_kernel(
                 window[b][:].indirect(entries(slot_sb, lo, hi)), kept[b][:, lo:hi], added[b][:, lo:hi], ALU.add
             )
 
-        blend(0, 0, HALF)
-        put(0, 0, HALF)
-        blend(0, HALF, S)
-        blend(1, 0, S)
-        put(0, HALF, S)
+        a, bb, c = PIECES
+        for piece in PIECES:
+            interleave(*piece)
+        quantise(*a)
+        gates(0, [a])
+        nc.vector.tensor_copy(old[:, 0:256], window[0][:].indirect(entries(slot_sb, 0, 256)))
+        quantise(*bb)
+        gates(0, [bb])
+        nc.vector.tensor_copy(old[:, 256:512], window[0][:].indirect(entries(slot_sb, 256, 512)))
+        quantise(*c)
+        gates(0, [c])
+        gates(1, PIECES)
+        keep_part(*a)
+        add_part(0, *a)
+        keep_part(*bb)
+        add_part(0, *bb)
+        put(0, *a)
+        keep_part(*c)
+        add_part(0, *c)
+        put(0, *bb)
+        nc.vector.tensor_tensor(kept[1][:], window[1][:].indirect(slot_sb[:]), keep_gate[1][:], ALU.mult)
+        add_part(1, 0, S)
+        put(0, *c)
         nc.sync.dma_start(out[0:P, :], window[0][:])
         put(1, 0, S)
         nc.sync.dma_start(out[P : 2 * P, :], window[1][:])

@@ -73,10 +73,10 @@ def tile_picked_gmem_tanh_e_kernel(
         x_codes = {lo: keep.tile([P, hi - lo], U32, name="x_codes%d" % lo, align_bytes=64) for lo, hi in PIECES}
         x_bytes = {lo: keep.tile([P, hi - lo], U8, name="x_bytes%d" % lo, align_bytes=64) for lo, hi in PIECES}
         old = keep.tile([P, S], F32, name="old")
-        keep_gate = [keep.tile([P, S], F32, name="keep_gate%d" % b) for b in range(2)]
-        neg_cand = [keep.tile([P, S], F32, name="neg_cand%d" % b) for b in range(2)]
-        kept = [keep.tile([P, S], F32, name="kept%d" % b) for b in range(2)]
-        added = [keep.tile([P, S], F32, name="added%d" % b) for b in range(2)]
+        keep_gate = keep.tile([P, 2 * S], F32, name="keep_gate")
+        neg_cand = keep.tile([P, 2 * S], F32, name="neg_cand")
+        kept = keep.tile([P, 2 * S], F32, name="kept")
+        added = keep.tile([P, 2 * S], F32, name="added")
 
         def interleave(lo, hi):
             nc.scalar.copy(
@@ -91,10 +91,15 @@ def tile_picked_gmem_tanh_e_kernel(
                 in_=grouped[lo][:].rearrange("p c t -> p (c t)"),
             )
 
-        def gates(b, pieces):
+        def gates(b, pieces, order, banks):
             first, last = pieces[0][0], pieces[-1][1]
-            acc = [psum.tile([P, last - first], F32, name="acc%d_%d_%d" % (i, b, first)) for i in range(2)]
-            for i in (GATE, CAND):
+            width = last - first
+            if banks == 2:
+                acc = [psum.tile([P, width], F32, name="acc%d_%d_%d" % (i, b, first))[:] for i in range(2)]
+            else:
+                both = psum.tile([P, 2 * width], F32, name="acc_%d_%d" % (b, first))
+                acc = [both[:, i * width : (i + 1) * width] for i in range(2)]
+            for i in order:
                 for lo, hi in pieces:
                     nc.tensor.matmul_mx(
                         out=acc[i][:, lo - first : hi - first],
@@ -105,44 +110,50 @@ def tile_picked_gmem_tanh_e_kernel(
                         start=True,
                         stop=True,
                     )
-            nc.scalar.activation(keep_gate[b][:, first:last], acc[GATE][:], ACT.Sigmoid, scale=-1.0)
-            nc.scalar.activation(neg_cand[b][:, first:last], acc[CAND][:], ACT.Tanh, scale=-1.0)
+            cols = slice(b * S + first, b * S + last)
+            for i in order:
+                if i == GATE:
+                    nc.scalar.activation(keep_gate[:, cols], acc[GATE], ACT.Sigmoid, scale=-1.0)
+                else:
+                    nc.scalar.activation(neg_cand[:, cols], acc[CAND], ACT.Tanh, scale=-1.0)
 
         def keep_part(lo, hi):
-            nc.vector.tensor_tensor(kept[0][:, lo:hi], old[:, lo:hi], keep_gate[0][:, lo:hi], ALU.mult)
+            nc.vector.tensor_tensor(kept[:, lo:hi], old[:, lo:hi], keep_gate[:, lo:hi], ALU.mult)
 
-        def add_part(b, lo, hi):
+        def add_part(lo, hi):
             nc.vector.scalar_tensor_tensor(
-                added[b][:, lo:hi], keep_gate[b][:, lo:hi], 1.0, neg_cand[b][:, lo:hi], ALU.subtract, ALU.mult
+                added[:, lo:hi], keep_gate[:, lo:hi], 1.0, neg_cand[:, lo:hi], ALU.subtract, ALU.mult
             )
 
         def put(b, lo, hi):
+            cols = slice(b * S + lo, b * S + hi)
             nc.vector.tensor_tensor(
-                window[b][:].indirect(entries(slot_sb, lo, hi)), kept[b][:, lo:hi], added[b][:, lo:hi], ALU.add
+                window[b][:].indirect(entries(slot_sb, lo, hi)), kept[:, cols], added[:, cols], ALU.add
             )
 
         a, bb, c = PIECES
+        LAP = LIST_ROWS
         for piece in PIECES:
             interleave(*piece)
         quantise(*a)
-        gates(0, [a])
-        nc.vector.tensor_copy(old[:, 0:256], window[0][:].indirect(entries(slot_sb, 0, 256)))
         quantise(*bb)
-        gates(0, [bb])
-        nc.vector.tensor_copy(old[:, 256:512], window[0][:].indirect(entries(slot_sb, 256, 512)))
+        gates(0, [a, bb], (GATE, CAND), 2)
+        nc.vector.tensor_copy(old[:, 0:384], window[0][:].indirect(entries(slot_sb, 0, 384)))
         quantise(*c)
-        gates(0, [c])
-        gates(1, PIECES)
-        keep_part(*a)
-        add_part(0, *a)
-        keep_part(*bb)
-        add_part(0, *bb)
+        old_last = keep.tile([P, 128], F32, name="picked")
+        nc.vector.tensor_copy(old_last[:], window[0][:].indirect(entries(slot_sb, 384, 512)))
+        gates(0, [c], (CAND, GATE), 2)
+        gates(1, PIECES, (CAND, GATE), 2)
+        keep_part(0, 256 - LAP)
+        add_part(*a)
+        add_part(*bb)
         put(0, *a)
-        keep_part(*c)
-        add_part(0, *c)
+        keep_part(256 - LAP, 384)
+        nc.vector.tensor_tensor(kept[:, 384:S], old_last[:], keep_gate[:, 384:S], ALU.mult)
+        add_part(256, S - LAP)
         put(0, *bb)
-        nc.vector.tensor_tensor(kept[1][:], window[1][:].indirect(slot_sb[:]), keep_gate[1][:], ALU.mult)
-        add_part(1, 0, S)
+        add_part(S - LAP, 2 * S)
+        nc.vector.tensor_tensor(kept[:, S : 2 * S], window[1][:].indirect(slot_sb[:]), keep_gate[:, S : 2 * S], ALU.mult)
         put(0, *c)
         nc.sync.dma_start(out[0:P, :], window[0][:])
         put(1, 0, S)

@@ -32,47 +32,60 @@ def tile_picked_gmem_tanh_e_kernel(
 
         offs_sb = keep.tile([P, S // LIST_ROWS], U16, name="offs_sb")
         slot_sb = keep.tile([P, S // LIST_ROWS], U16, name="slot_sb")
-        x_rows = [keep.tile([P, T], F32, name="x_row%d" % j) for j in range(PACK)]
+        x_rows = [keep.tile([P, T], F32, name="x_row%d" % j, align_bytes=64) for j in range(PACK)]
         window = [keep.tile([P, U], F32, name="window%d" % b) for b in range(2)]
         w_codes = [keep.tile([P, N], U32, name="w_codes%d" % i, align_bytes=64) for i in range(2)]
-        w_bytes = [keep.tile([P, N], U8, name="w_bytes%d" % i, align_bytes=64) for i in range(2)]
+        w_bytes = {GATE: keep.tile([P, N], U8, name="gate_bytes", align_bytes=64)}
         warm = keep.tile([P, 2], F32, name="warm")
 
         def entries(lst, lo, hi):
             return lst[:, lo // LIST_ROWS : hi // LIST_ROWS]
 
-        for i in (GATE, CAND):
-            nc.vector.memset(w_bytes[i][:].bitcast(I32), 0)
+        nc.vector.memset(w_bytes[GATE][:].bitcast(I32), 0)
         nc.vector.memset(warm[:, 0:1], 0.0)
 
         x_view = xT.rearrange("(p j) t -> p j t", j=PACK)
+
+        def load_words(i, words):
+            nc.sync.dma_start(w_codes[i][:].bitcast(I32), words[0].rearrange("p n t -> p (n t)").bitcast(I32))
+
+        def load_scales(queue, i, scales, q):
+            queue.dma_start(
+                w_bytes[i][32 * q : 32 * q + 4, :].bitcast(I32), scales[0, 4 * q : 4 * q + 4, :].bitcast(I32)
+            )
+
         nc.sync.dma_start(x_rows[0][:], x_view[:, 0, :])
         nc.sync.dma_start(offs_sb[:], offs)
-        for j in range(1, PACK - 1):
-            nc.sync.dma_start(x_rows[j][:], x_view[:, j, :])
+        nc.sync.dma_start(x_rows[1][:], x_view[:, 1, :])
+        nc.sync.dma_start(x_rows[2][:], x_view[:, 2, :])
+        nc.sync.dma_start(x_rows[3][:], x_view[:, 3, :])
         nc.sync.dma_start(slot_sb[:], slot)
-        nc.sync.dma_start(x_rows[PACK - 1][:], x_view[:, PACK - 1, :])
-        for i, words in ((GATE, w2_words), (CAND, w1_words)):
-            nc.sync.dma_start(w_codes[i][:].bitcast(I32), words[0].rearrange("p n t -> p (n t)").bitcast(I32))
         nc.sync.dma_start(window[0][:], mem[0:P, :])
+        load_words(GATE, w2_words)
+        load_words(CAND, w1_words)
         nc.sync.dma_start(window[1][:], mem[P : 2 * P, :])
-        for i, scales in ((GATE, w2_scales), (CAND, w1_scales)):
-            for q in range(4):
-                nc.scalar.dma_start(
-                    w_bytes[i][32 * q : 32 * q + 4, :].bitcast(I32), scales[0, 4 * q : 4 * q + 4, :].bitcast(I32)
-                )
+        load_scales(nc.scalar, GATE, w2_scales, 0)
+        load_scales(nc.scalar, GATE, w2_scales, 1)
+        load_scales(nc.scalar, GATE, w2_scales, 2)
+        load_scales(nc.scalar, GATE, w2_scales, 3)
         nc.scalar.activation(warm[:, 1:2], warm[:, 0:1], ACT.Sigmoid)
 
-        picked = keep.tile([P, PACK, S], BF16, name="picked")
+        PAD = 2 * S - 256
+        shared = keep.tile([P, PAD + PACK * S], BF16, name="shared")
+        picked = shared[:, PAD : PAD + PACK * S].rearrange("p (t s) -> p t s", t=PACK)
+        old = shared[:, 0 : 2 * S].bitcast(F32)
         for j in range(PACK - 1):
             nc.vector.tensor_copy(picked[:, j, :], x_rows[j][:].indirect(offs_sb[:]))
+        w_bytes[CAND] = keep.tile([P, N], U8, name="x_row1", align_bytes=64)
+        nc.gpsimd.memset(w_bytes[CAND][:].bitcast(I32), 0)
+        for q in range(4):
+            load_scales(nc.scalar, CAND, w1_scales, q)
         for lo, hi in PIECES:
             nc.vector.tensor_copy(picked[:, PACK - 1, lo:hi], x_rows[PACK - 1][:].indirect(entries(offs_sb, lo, hi)))
 
         grouped = {lo: keep.tile([P, hi - lo, PACK], BF16, name="grouped%d" % lo, align_bytes=64) for lo, hi in PIECES}
         x_codes = {lo: keep.tile([P, hi - lo], U32, name="x_codes%d" % lo, align_bytes=64) for lo, hi in PIECES}
         x_bytes = {lo: keep.tile([P, hi - lo], U8, name="x_bytes%d" % lo, align_bytes=64) for lo, hi in PIECES}
-        old = keep.tile([P, S], F32, name="old")
         keep_gate = keep.tile([P, 2 * S], F32, name="keep_gate")
         neg_cand = keep.tile([P, 2 * S], F32, name="neg_cand")
         kept = keep.tile([P, 2 * S], F32, name="kept")
@@ -135,21 +148,19 @@ def tile_picked_gmem_tanh_e_kernel(
         LAP = LIST_ROWS
         for piece in PIECES:
             interleave(*piece)
+        nc.vector.tensor_copy(old[:, 0:128], window[0][:].indirect(entries(slot_sb, 0, 128)))
         quantise(*a)
         quantise(*bb)
         gates(0, [a, bb], (GATE, CAND), 2)
-        nc.vector.tensor_copy(old[:, 0:384], window[0][:].indirect(entries(slot_sb, 0, 384)))
+        nc.vector.tensor_copy(old[:, 128:512], window[0][:].indirect(entries(slot_sb, 128, 512)))
         quantise(*c)
-        old_last = keep.tile([P, 128], F32, name="picked")
-        nc.vector.tensor_copy(old_last[:], window[0][:].indirect(entries(slot_sb, 384, 512)))
         gates(0, [c], (CAND, GATE), 2)
         gates(1, PIECES, (CAND, GATE), 2)
         keep_part(0, 256 - LAP)
         add_part(*a)
         add_part(*bb)
         put(0, *a)
-        keep_part(256 - LAP, 384)
-        nc.vector.tensor_tensor(kept[:, 384:S], old_last[:], keep_gate[:, 384:S], ALU.mult)
+        keep_part(256 - LAP, S)
         add_part(256, S - LAP)
         put(0, *bb)
         add_part(S - LAP, 2 * S)

@@ -152,10 +152,11 @@ def tile_picked_gmem_tanh_e_kernel(
         quantise(*a)
         quantise(*bb)
         gates(0, [a, bb], (GATE, CAND), 2)
+        gates(1, [a, bb], (CAND, GATE), 1)
         nc.vector.tensor_copy(old[:, 128:512], window[0][:].indirect(entries(slot_sb, 128, 512)))
         quantise(*c)
-        gates(0, [c], (CAND, GATE), 2)
-        gates(1, PIECES, (CAND, GATE), 2)
+        gates(0, [c], (GATE, CAND), 2)
+        gates(1, [c], (CAND, GATE), 2)
         keep_part(0, 256 - LAP)
         add_part(*a)
         add_part(*bb)

@@ -20,6 +20,7 @@ PACK = 4
 LIST_ROWS = 16
 PIECES = ((0, 128), (128, 256), (256, 512))
 CAND, GATE = 0, 1
+HALF = S // 2
 
 
 def tile_picked_gmem_tanh_e_kernel(
@@ -62,8 +63,8 @@ def tile_picked_gmem_tanh_e_kernel(
         nc.sync.dma_start(slot_sb[:], slot)
         nc.sync.dma_start(window[0][:], mem[0:P, :])
         load_words(GATE, w2_words)
-        load_words(CAND, w1_words)
         nc.sync.dma_start(window[1][:], mem[P : 2 * P, :])
+        load_words(CAND, w1_words)
         load_scales(nc.scalar, GATE, w2_scales, 0)
         load_scales(nc.scalar, GATE, w2_scales, 1)
         load_scales(nc.scalar, GATE, w2_scales, 2)
@@ -104,31 +105,34 @@ def tile_picked_gmem_tanh_e_kernel(
                 in_=grouped[lo][:].rearrange("p c t -> p (c t)"),
             )
 
-        def gates(b, pieces, order, banks):
-            first, last = pieces[0][0], pieces[-1][1]
-            width = last - first
-            if banks == 2:
-                acc = [psum.tile([P, width], F32, name="acc%d_%d_%d" % (i, b, first))[:] for i in range(2)]
+        def products(b, i, pieces, acc):
+            first = pieces[0][0]
+            for lo, hi in pieces:
+                nc.tensor.matmul_mx(
+                    out=acc[:, lo - first : hi - first],
+                    lhsT=w_codes[i][:, b * P : (b + 1) * P].bitcast(FP8X4),
+                    lhsT_scale=w_bytes[i][:, b * P : (b + 1) * P],
+                    rhs=x_codes[lo][:].bitcast(FP8X4),
+                    rhs_scale=x_bytes[lo][:],
+                    start=True,
+                    stop=True,
+                )
+
+        def activate(b, i, first, acc):
+            cols = slice(b * S + first, b * S + first + HALF)
+            if i == GATE:
+                nc.scalar.activation(keep_gate[:, cols], acc, ACT.Sigmoid, scale=-1.0)
             else:
-                both = psum.tile([P, 2 * width], F32, name="acc_%d_%d" % (b, first))
-                acc = [both[:, i * width : (i + 1) * width] for i in range(2)]
-            for i in order:
-                for lo, hi in pieces:
-                    nc.tensor.matmul_mx(
-                        out=acc[i][:, lo - first : hi - first],
-                        lhsT=w_codes[i][:, b * P : (b + 1) * P].bitcast(FP8X4),
-                        lhsT_scale=w_bytes[i][:, b * P : (b + 1) * P],
-                        rhs=x_codes[lo][:].bitcast(FP8X4),
-                        rhs_scale=x_bytes[lo][:],
-                        start=True,
-                        stop=True,
-                    )
-            cols = slice(b * S + first, b * S + last)
-            for i in order:
-                if i == GATE:
-                    nc.scalar.activation(keep_gate[:, cols], acc[GATE], ACT.Sigmoid, scale=-1.0)
-                else:
-                    nc.scalar.activation(neg_cand[:, cols], acc[CAND], ACT.Tanh, scale=-1.0)
+                nc.scalar.activation(neg_cand[:, cols], acc, ACT.Tanh, scale=-1.0)
+
+        def bank(name, width):
+            return psum.tile([P, width], F32, name=name)[:]
+
+        def keep_gathered(lo, hi):
+            cols = slice(S + lo, S + hi)
+            nc.vector.tensor_tensor(
+                kept[:, cols], window[1][:].indirect(entries(slot_sb, lo, hi)), keep_gate[:, cols], ALU.mult
+            )
 
         def keep_part(lo, hi):
             nc.vector.tensor_tensor(kept[:, lo:hi], old[:, lo:hi], keep_gate[:, lo:hi], ALU.mult)
@@ -145,28 +149,33 @@ def tile_picked_gmem_tanh_e_kernel(
             )
 
         a, bb, c = PIECES
-        LAP = LIST_ROWS
         for piece in PIECES:
             interleave(*piece)
         nc.vector.tensor_copy(old[:, 0:128], window[0][:].indirect(entries(slot_sb, 0, 128)))
         quantise(*a)
         quantise(*bb)
-        gates(0, [a, bb], (GATE, CAND), 2)
-        gates(1, [a, bb], (CAND, GATE), 1)
+        late = [bank("late%d" % b, S) for b in range(2)]
+        for i in (GATE, CAND):
+            for b in range(2):
+                acc = late[b][:, 0:HALF] if i == CAND else bank("gate%d" % b, HALF)
+                products(b, i, [a, bb], acc)
+                activate(b, i, 0, acc)
         nc.vector.tensor_copy(old[:, 128:512], window[0][:].indirect(entries(slot_sb, 128, 512)))
         quantise(*c)
-        gates(0, [c], (GATE, CAND), 2)
-        gates(1, [c], (CAND, GATE), 2)
-        keep_part(0, 256 - LAP)
-        add_part(*a)
-        add_part(*bb)
-        put(0, *a)
-        keep_part(256 - LAP, S)
-        add_part(256, S - LAP)
-        put(0, *bb)
-        add_part(S - LAP, 2 * S)
-        nc.vector.tensor_tensor(kept[:, S : 2 * S], window[1][:].indirect(slot_sb[:]), keep_gate[:, S : 2 * S], ALU.mult)
-        put(0, *c)
+        for b, i in ((0, GATE), (0, CAND), (1, CAND), (1, GATE)):
+            acc = late[b][:, HALF:S] if i == GATE else bank("cand%d" % b, HALF)
+            products(b, i, [c], acc)
+            activate(b, i, HALF, acc)
+        keep_part(0, HALF)
+        keep_gathered(0, HALF)
+        add_part(0, HALF)
+        add_part(S, S + HALF)
+        put(0, 0, HALF)
+        keep_part(HALF, S)
+        backs = [t[:].rearrange("p (b s) -> p b s", b=2)[:, :, HALF:S] for t in (added, keep_gate, neg_cand)]
+        nc.vector.scalar_tensor_tensor(backs[0], backs[1], 1.0, backs[2], ALU.subtract, ALU.mult)
+        keep_gathered(HALF, S)
+        put(0, HALF, S)
         nc.sync.dma_start(out[0:P, :], window[0][:])
         put(1, 0, S)
         nc.sync.dma_start(out[P : 2 * P, :], window[1][:])

@@ -42,7 +42,6 @@ def tile_picked_gmem_tanh_e_kernel(
         def entries(lst, lo, hi):
             return lst[:, lo // LIST_ROWS : hi // LIST_ROWS]
 
-        nc.vector.memset(w_bytes[GATE][:].bitcast(I32), 0)
         nc.vector.memset(warm[:, 0:1], 0.0)
 
         x_view = xT.rearrange("(p j) t -> p j t", j=PACK)

@@ -1,6 +1,7 @@
 from contextlib import ExitStack
 
 import concourse.mybir as mybir
+from concourse.masks import make_identity
 
 K, T, S, N, U = 512, 1024, 512, 256, 1024
 FLOPS = 2 * 2 * K * N * S
@@ -74,22 +75,32 @@ def tile_picked_gmem_tanh_e_kernel(
         shared = keep.tile([P, PAD + PACK * S], BF16, name="shared")
         picked = shared[:, PAD : PAD + PACK * S].rearrange("p (t s) -> p t s", t=PACK)
         old = shared[:, 0 : 2 * S].bitcast(F32)
-        for j in range(PACK - 1):
-            nc.vector.tensor_copy(picked[:, j, :], x_rows[j][:].indirect(offs_sb[:]))
+        rounded = keep.tile([P, T], BF16, name="rounded")
+        nc.vector.tensor_copy(picked[:, 0, :], x_rows[0][:].indirect(offs_sb[:]))
+        nc.vector.tensor_copy(rounded[:], x_rows[1][:])
+        nc.scalar.activation(picked[:, 1, :], rounded[:].indirect(offs_sb[:]), ACT.Copy)
+        nc.vector.tensor_copy(picked[:, 2, :], x_rows[2][:].indirect(offs_sb[:]))
         w_bytes[CAND] = keep.tile([P, N], U8, name="x_row1", align_bytes=64)
         nc.gpsimd.memset(w_bytes[CAND][:].bitcast(I32), 0)
         for q in range(4):
             load_scales(nc.scalar, CAND, w1_scales, q)
+        ident = keep.tile([P, P], F32, name="x_row2", align_bytes=64)
+        make_identity(nc, ident[:])
         for lo, hi in PIECES:
             nc.vector.tensor_copy(picked[:, PACK - 1, lo:hi], x_rows[PACK - 1][:].indirect(entries(offs_sb, lo, hi)))
 
         grouped = {lo: keep.tile([P, hi - lo, PACK], BF16, name="grouped%d" % lo, align_bytes=64) for lo, hi in PIECES}
         x_codes = {lo: keep.tile([P, hi - lo], U32, name="x_codes%d" % lo, align_bytes=64) for lo, hi in PIECES}
         x_bytes = {lo: keep.tile([P, hi - lo], U8, name="x_bytes%d" % lo, align_bytes=64) for lo, hi in PIECES}
-        keep_gate = keep.tile([P, 2 * S], F32, name="keep_gate")
-        neg_cand = keep.tile([P, 2 * S], F32, name="neg_cand")
-        kept = keep.tile([P, 2 * S], F32, name="kept")
-        added = keep.tile([P, 2 * S], F32, name="added")
+        keep_gate = keep.tile([P, 3 * HALF], F32, name="keep_gate")
+        neg_cand = keep.tile([P, 3 * HALF], F32, name="neg_cand")
+        kept = keep.tile([P, 3 * HALF], F32, name="kept")
+        added = keep.tile([P, 4 * HALF], F32, name="added")
+        LEAD = 64
+        gate = added[:, 3 * HALF - LEAD : 4 * HALF - LEAD]
+        cand_t = keep.tile([P, HALF], F32, name="cand_t")
+        neg_old_t = keep.tile([P, HALF], F32, name="neg_old_t")
+        pull = keep.tile([P, HALF], F32, name="pull")
 
         def interleave(lo, hi):
             nc.scalar.copy(
@@ -117,35 +128,14 @@ def tile_picked_gmem_tanh_e_kernel(
                     stop=True,
                 )
 
-        def activate(b, i, first, acc):
-            cols = slice(b * S + first, b * S + first + HALF)
-            if i == GATE:
-                nc.scalar.activation(keep_gate[:, cols], acc, ACT.Sigmoid, scale=-1.0)
-            else:
-                nc.scalar.activation(neg_cand[:, cols], acc, ACT.Tanh, scale=-1.0)
-
         def bank(name, width):
             return psum.tile([P, width], F32, name=name)[:]
 
-        def keep_gathered(lo, hi):
-            cols = slice(S + lo, S + hi)
-            nc.vector.tensor_tensor(
-                kept[:, cols], window[1][:].indirect(entries(slot_sb, lo, hi)), keep_gate[:, cols], ALU.mult
-            )
+        def half(b):
+            return slice(b * HALF, (b + 1) * HALF)
 
-        def keep_part(lo, hi):
-            nc.vector.tensor_tensor(kept[:, lo:hi], old[:, lo:hi], keep_gate[:, lo:hi], ALU.mult)
-
-        def add_part(lo, hi):
-            nc.vector.scalar_tensor_tensor(
-                added[:, lo:hi], keep_gate[:, lo:hi], 1.0, neg_cand[:, lo:hi], ALU.subtract, ALU.mult
-            )
-
-        def put(b, lo, hi):
-            cols = slice(b * S + lo, b * S + hi)
-            nc.vector.tensor_tensor(
-                window[b][:].indirect(entries(slot_sb, lo, hi)), kept[:, cols], added[:, cols], ALU.add
-            )
+        def put(b, lo, first, second):
+            nc.vector.tensor_tensor(window[b][:].indirect(entries(slot_sb, lo, lo + HALF)), first, second, ALU.add)
 
         a, bb, c = PIECES
         for piece in PIECES:
@@ -154,27 +144,71 @@ def tile_picked_gmem_tanh_e_kernel(
         quantise(*a)
         quantise(*bb)
         late = [bank("late%d" % b, S) for b in range(2)]
+
+        def activate(i, n, acc):
+            if i == GATE:
+                nc.scalar.activation(keep_gate[:, half(n)], acc, ACT.Sigmoid, scale=-1.0)
+            else:
+                nc.scalar.activation(neg_cand[:, half(n)], acc, ACT.Tanh, scale=-1.0)
+
+        def keep_gathered(n, lo):
+            nc.vector.tensor_tensor(
+                kept[:, half(n)], window[1][:].indirect(entries(slot_sb, lo, lo + HALF)), keep_gate[:, half(n)], ALU.mult
+            )
+
+        def add_part(n, dst):
+            nc.vector.scalar_tensor_tensor(dst, keep_gate[:, half(n)], 1.0, neg_cand[:, half(n)], ALU.subtract, ALU.mult)
+
         for i in (GATE, CAND):
             for b in range(2):
                 acc = late[b][:, 0:HALF] if i == CAND else bank("gate%d" % b, HALF)
                 products(b, i, [a, bb], acc)
-                activate(b, i, 0, acc)
+                activate(i, b, acc)
         nc.vector.tensor_copy(old[:, 128:512], window[0][:].indirect(entries(slot_sb, 128, 512)))
         quantise(*c)
-        for b, i in ((0, GATE), (0, CAND), (1, CAND), (1, GATE)):
-            acc = late[b][:, HALF:S] if i == GATE else bank("cand%d" % b, HALF)
-            products(b, i, [c], acc)
-            activate(b, i, HALF, acc)
-        keep_part(0, HALF)
-        keep_gathered(0, HALF)
-        add_part(0, HALF)
-        add_part(S, S + HALF)
-        put(0, 0, HALF)
-        keep_part(HALF, S)
-        backs = [t[:].rearrange("p (b s) -> p b s", b=2)[:, :, HALF:S] for t in (added, keep_gate, neg_cand)]
-        nc.vector.scalar_tensor_tensor(backs[0], backs[1], 1.0, backs[2], ALU.subtract, ALU.mult)
-        keep_gathered(HALF, S)
-        put(0, HALF, S)
+        products(1, GATE, [c], late[0][:, HALF:S])
+        activate(GATE, 2, late[0][:, HALF:S])
+        acc = bank("cand1", HALF)
+        products(1, CAND, [c], acc)
+        activate(CAND, 2, acc)
+
+        old_t = bank("cand1", HALF)
+        for at in (0, P):
+            nc.tensor.transpose(old_t[:, at : at + P], old[:, HALF + at : HALF + at + P], ident[:])
+        nc.scalar.activation(neg_old_t[:], old_t, ACT.Copy, scale=-1.0)
+        turned = bank("turned", HALF)
+        for at in (0, P):
+            nc.tensor.matmul_mx(
+                out=turned[:, at : at + P],
+                lhsT=x_codes[HALF][:, at : at + P].bitcast(FP8X4),
+                lhsT_scale=x_bytes[HALF][:, at : at + P],
+                rhs=w_codes[CAND][:, 0:P].bitcast(FP8X4),
+                rhs_scale=w_bytes[CAND][:, 0:P],
+                start=True,
+                stop=True,
+            )
+        nc.scalar.activation(cand_t[:], turned, ACT.Tanh)
+        acc = late[1][:, HALF:S]
+        products(0, GATE, [c], acc)
+        nc.scalar.activation(gate, acc, ACT.Sigmoid)
+        diff = bank("diff", HALF)
+        for at in (0, P):
+            cols = slice(at, at + P)
+            nc.tensor.matmul(diff[:, cols], neg_old_t[:, cols], ident[:], start=True, stop=False, is_transpose=True)
+            nc.tensor.matmul(diff[:, cols], cand_t[:, cols], ident[:], start=False, stop=True, is_transpose=True)
+
+        nc.vector.tensor_tensor(kept[:, half(0)], old[:, 0:HALF], keep_gate[:, half(0)], ALU.mult)
+        keep_gathered(1, 0)
+        add_part(0, added[:, half(0)])
+        add_part(1, added[:, half(1)])
+        put(0, 0, kept[:, half(0)], added[:, half(0)])
+        keep_gathered(2, HALF)
+        for lo, hi in ((0, LEAD), (LEAD, HALF)):
+            nc.vector.tensor_tensor(pull[:, lo:hi], diff[:, lo:hi], gate[:, lo:hi], ALU.mult)
+        add_part(2, added[:, half(2)])
+        put(0, HALF, pull[:], old[:, HALF:S])
         nc.sync.dma_start(out[0:P, :], window[0][:])
-        put(1, 0, S)
+        nc.vector.tensor_tensor(
+            window[1][:].indirect(slot_sb[:]), kept[:, HALF : 3 * HALF], added[:, HALF : 3 * HALF], ALU.add
+        )
         nc.sync.dma_start(out[P : 2 * P, :], window[1][:])

@@ -44,6 +44,8 @@ def tile_picked_gmem_tanh_e_kernel(
             return lst[:, lo // LIST_ROWS : hi // LIST_ROWS]
 
         nc.vector.memset(warm[:, 0:1], 0.0)
+        ident = keep.tile([P, P], F32, name="ident")
+        make_identity(nc, ident[:])
 
         x_view = xT.rearrange("(p j) t -> p j t", j=PACK)
 
@@ -81,11 +83,8 @@ def tile_picked_gmem_tanh_e_kernel(
         nc.scalar.activation(picked[:, 1, :], rounded[:].indirect(offs_sb[:]), ACT.Copy)
         nc.vector.tensor_copy(picked[:, 2, :], x_rows[2][:].indirect(offs_sb[:]))
         w_bytes[CAND] = keep.tile([P, N], U8, name="x_row1", align_bytes=64)
-        nc.gpsimd.memset(w_bytes[CAND][:].bitcast(I32), 0)
         for q in range(4):
             load_scales(nc.scalar, CAND, w1_scales, q)
-        ident = keep.tile([P, P], F32, name="x_row2", align_bytes=64)
-        make_identity(nc, ident[:])
         for lo, hi in PIECES:
             nc.vector.tensor_copy(picked[:, PACK - 1, lo:hi], x_rows[PACK - 1][:].indirect(entries(offs_sb, lo, hi)))
 

@@ -91,15 +91,15 @@ def tile_picked_gmem_tanh_e_kernel(
         grouped = {lo: keep.tile([P, hi - lo, PACK], BF16, name="grouped%d" % lo, align_bytes=64) for lo, hi in PIECES}
         x_codes = {lo: keep.tile([P, hi - lo], U32, name="x_codes%d" % lo, align_bytes=64) for lo, hi in PIECES}
         x_bytes = {lo: keep.tile([P, hi - lo], U8, name="x_bytes%d" % lo, align_bytes=64) for lo, hi in PIECES}
-        keep_gate = keep.tile([P, 3 * HALF], F32, name="keep_gate")
-        neg_cand = keep.tile([P, 3 * HALF], F32, name="neg_cand")
-        kept = keep.tile([P, 3 * HALF], F32, name="kept")
-        added = keep.tile([P, 4 * HALF], F32, name="added")
-        LEAD = 64
-        gate = added[:, 3 * HALF - LEAD : 4 * HALF - LEAD]
-        cand_t = keep.tile([P, HALF], F32, name="cand_t")
-        neg_old_t = keep.tile([P, HALF], F32, name="neg_old_t")
-        pull = keep.tile([P, HALF], F32, name="pull")
+        keep_gate = keep.tile([P, S], F32, name="keep_gate")
+        neg_cand = keep.tile([P, S], F32, name="neg_cand")
+        kept = keep.tile([P, S], F32, name="kept")
+        added = keep.tile([P, S], F32, name="added")
+        gate = keep.tile([P, S], F32, name="gate")
+        cand_t = keep.tile([P, S], F32, name="cand_t")
+        neg_old_t = keep.tile([P, S], F32, name="neg_old_t")
+        pull = keep.tile([P, S], F32, name="pull")
+        old1 = keep.tile([P, HALF], F32, name="old1")
 
         def interleave(lo, hi):
             nc.scalar.copy(
@@ -142,72 +142,62 @@ def tile_picked_gmem_tanh_e_kernel(
         nc.vector.tensor_copy(old[:, 0:128], window[0][:].indirect(entries(slot_sb, 0, 128)))
         quantise(*a)
         quantise(*bb)
-        late = [bank("late%d" % b, S) for b in range(2)]
-
-        def activate(i, n, acc):
-            if i == GATE:
-                nc.scalar.activation(keep_gate[:, half(n)], acc, ACT.Sigmoid, scale=-1.0)
-            else:
-                nc.scalar.activation(neg_cand[:, half(n)], acc, ACT.Tanh, scale=-1.0)
-
-        def keep_gathered(n, lo):
-            nc.vector.tensor_tensor(
-                kept[:, half(n)], window[1][:].indirect(entries(slot_sb, lo, lo + HALF)), keep_gate[:, half(n)], ALU.mult
-            )
-
-        def add_part(n, dst):
-            nc.vector.scalar_tensor_tensor(dst, keep_gate[:, half(n)], 1.0, neg_cand[:, half(n)], ALU.subtract, ALU.mult)
-
         for i in (GATE, CAND):
             for b in range(2):
-                acc = late[b][:, 0:HALF] if i == CAND else bank("gate%d" % b, HALF)
+                acc = bank("first%d_%d" % (i, b), HALF)
                 products(b, i, [a, bb], acc)
-                activate(i, b, acc)
+                if i == GATE:
+                    nc.scalar.activation(keep_gate[:, half(b)], acc, ACT.Sigmoid, scale=-1.0)
+                else:
+                    nc.scalar.activation(neg_cand[:, half(b)], acc, ACT.Tanh, scale=-1.0)
         nc.vector.tensor_copy(old[:, 128:512], window[0][:].indirect(entries(slot_sb, 128, 512)))
         quantise(*c)
-        products(1, GATE, [c], late[0][:, HALF:S])
-        activate(GATE, 2, late[0][:, HALF:S])
-        acc = bank("cand1", HALF)
-        products(1, CAND, [c], acc)
-        activate(CAND, 2, acc)
+        nc.vector.tensor_copy(old1[:], window[1][:].indirect(entries(slot_sb, HALF, S)))
+        nc.vector.tensor_tensor(kept[:, half(0)], old[:, 0:HALF], keep_gate[:, half(0)], ALU.mult)
+        nc.vector.tensor_tensor(
+            kept[:, half(1)], window[1][:].indirect(entries(slot_sb, 0, HALF)), keep_gate[:, half(1)], ALU.mult
+        )
+        for b in range(2):
+            nc.vector.scalar_tensor_tensor(
+                added[:, half(b)], keep_gate[:, half(b)], 1.0, neg_cand[:, half(b)], ALU.subtract, ALU.mult
+            )
+        late_old = [old[:, HALF:S], old1[:]]
 
-        old_t = bank("cand1", HALF)
-        for at in (0, P):
-            nc.tensor.transpose(old_t[:, at : at + P], old[:, HALF + at : HALF + at + P], ident[:])
-        nc.scalar.activation(neg_old_t[:], old_t, ACT.Copy, scale=-1.0)
-        turned = bank("turned", HALF)
-        for at in (0, P):
+        turned = bank("turned", S)
+        for t in range(2):
+            cols = slice(t * P, (t + 1) * P)
             nc.tensor.matmul_mx(
-                out=turned[:, at : at + P],
-                lhsT=x_codes[HALF][:, at : at + P].bitcast(FP8X4),
-                lhsT_scale=x_bytes[HALF][:, at : at + P],
-                rhs=w_codes[CAND][:, 0:P].bitcast(FP8X4),
-                rhs_scale=w_bytes[CAND][:, 0:P],
+                out=turned[:, half(t)],
+                lhsT=x_codes[HALF][:, cols].bitcast(FP8X4),
+                lhsT_scale=x_bytes[HALF][:, cols],
+                rhs=w_codes[CAND][:].bitcast(FP8X4),
+                rhs_scale=w_bytes[CAND][:],
                 start=True,
                 stop=True,
             )
         nc.scalar.activation(cand_t[:], turned, ACT.Tanh)
-        acc = late[1][:, HALF:S]
-        products(0, GATE, [c], acc)
-        nc.scalar.activation(gate, acc, ACT.Sigmoid)
-        diff = bank("diff", HALF)
-        for at in (0, P):
-            cols = slice(at, at + P)
-            nc.tensor.matmul(diff[:, cols], neg_old_t[:, cols], ident[:], start=True, stop=False, is_transpose=True)
-            nc.tensor.matmul(diff[:, cols], cand_t[:, cols], ident[:], start=False, stop=True, is_transpose=True)
+        acc = bank("first%d_0" % CAND, S)
+        for b in range(2):
+            products(b, GATE, [c], acc[:, half(b)])
+        nc.scalar.activation(gate[:], acc, ACT.Sigmoid)
+        old_t = bank("first%d_1" % CAND, S)
+        for b in range(2):
+            for t in range(2):
+                at = t * HALF + b * P
+                nc.tensor.transpose(old_t[:, at : at + P], late_old[b][:, t * P : (t + 1) * P], ident[:])
+        nc.scalar.activation(neg_old_t[:], old_t, ACT.Copy, scale=-1.0)
+        diff = bank("diff", S)
+        for b in range(2):
+            for t in range(2):
+                src = slice(t * HALF + b * P, t * HALF + (b + 1) * P)
+                dst = slice(b * HALF + t * P, b * HALF + (t + 1) * P)
+                nc.tensor.matmul(diff[:, dst], neg_old_t[:, src], ident[:], start=True, stop=False, is_transpose=True)
+                nc.tensor.matmul(diff[:, dst], cand_t[:, src], ident[:], start=False, stop=True, is_transpose=True)
 
-        nc.vector.tensor_tensor(kept[:, half(0)], old[:, 0:HALF], keep_gate[:, half(0)], ALU.mult)
-        keep_gathered(1, 0)
-        add_part(0, added[:, half(0)])
-        add_part(1, added[:, half(1)])
         put(0, 0, kept[:, half(0)], added[:, half(0)])
-        keep_gathered(2, HALF)
-        for lo, hi in ((0, LEAD), (LEAD, HALF)):
-            nc.vector.tensor_tensor(pull[:, lo:hi], diff[:, lo:hi], gate[:, lo:hi], ALU.mult)
-        add_part(2, added[:, half(2)])
-        put(0, HALF, pull[:], old[:, HALF:S])
-        nc.sync.dma_start(out[0:P, :], window[0][:])
-        nc.vector.tensor_tensor(
-            window[1][:].indirect(slot_sb[:]), kept[:, HALF : 3 * HALF], added[:, HALF : 3 * HALF], ALU.add
-        )
-        nc.sync.dma_start(out[P : 2 * P, :], window[1][:])
+        put(1, 0, kept[:, half(1)], added[:, half(1)])
+        for b in range(2):
+            nc.vector.tensor_tensor(pull[:, half(b)], diff[:, half(b)], gate[:, half(b)], ALU.mult)
+        for b in range(2):
+            put(b, HALF, pull[:, half(b)], late_old[b])
+            nc.sync.dma_start(out[b * P : (b + 1) * P, :], window[b][:])

@@ -74,21 +74,21 @@ def tile_picked_gmem_tanh_e_kernel(
         nc.scalar.activation(warm[:, 1:2], warm[:, 0:1], ACT.Sigmoid)
 
         PAD = 2 * S - 256
-        shared = keep.tile([P, PAD + PACK * S], BF16, name="shared")
-        picked = shared[:, PAD : PAD + PACK * S].rearrange("p (t s) -> p t s", t=PACK)
+        shared = keep.tile([P, PAD + 2 * S], BF16, name="shared")
+        picked = shared[:, PAD : PAD + 2 * S].rearrange("p (t s) -> p t s", t=2)
         old = shared[:, 0 : 2 * S].bitcast(F32)
-        rounded = keep.tile([P, T], BF16, name="rounded")
-        nc.vector.tensor_copy(picked[:, 0, :], x_rows[0][:].indirect(offs_sb[:]))
-        nc.vector.tensor_copy(rounded[:], x_rows[1][:])
-        nc.scalar.activation(picked[:, 1, :], rounded[:].indirect(offs_sb[:]), ACT.Copy)
-        nc.vector.tensor_copy(picked[:, 2, :], x_rows[2][:].indirect(offs_sb[:]))
+        grouped = keep.tile([P, S, PACK], BF16, name="grouped", align_bytes=64)
+        for j in range(2):
+            rounded = keep.tile([P, T], BF16, name="rounded%d" % j)
+            nc.vector.tensor_copy(rounded[:], x_rows[j][:])
+            nc.scalar.activation(grouped[:, :, j], rounded[:].indirect(offs_sb[:]), ACT.Copy)
+        nc.vector.tensor_copy(picked[:, 0, :], x_rows[2][:].indirect(offs_sb[:]))
         w_bytes[CAND] = keep.tile([P, N], U8, name="x_row1", align_bytes=64)
         for q in range(4):
             load_scales(nc.scalar, CAND, w1_scales, q)
         for lo, hi in PIECES:
-            nc.vector.tensor_copy(picked[:, PACK - 1, lo:hi], x_rows[PACK - 1][:].indirect(entries(offs_sb, lo, hi)))
+            nc.vector.tensor_copy(picked[:, 1, lo:hi], x_rows[PACK - 1][:].indirect(entries(offs_sb, lo, hi)))
 
-        grouped = {lo: keep.tile([P, hi - lo, PACK], BF16, name="grouped%d" % lo, align_bytes=64) for lo, hi in PIECES}
         x_codes = {lo: keep.tile([P, hi - lo], U32, name="x_codes%d" % lo, align_bytes=64) for lo, hi in PIECES}
         x_bytes = {lo: keep.tile([P, hi - lo], U8, name="x_bytes%d" % lo, align_bytes=64) for lo, hi in PIECES}
         keep_gate = keep.tile([P, S], F32, name="keep_gate")
@@ -103,15 +103,15 @@ def tile_picked_gmem_tanh_e_kernel(
 
         def interleave(lo, hi):
             nc.scalar.copy(
-                grouped[lo][:].rearrange("p (c i) t -> p c t i", i=4),
-                picked[:, :, lo:hi].rearrange("p t (c i) -> p c t i", i=4),
+                grouped[:, lo:hi, 2:PACK],
+                picked[:, :, lo:hi].rearrange("p t s -> p s t"),
             )
 
         def quantise(lo, hi):
             nc.vector.quantize_mx(
                 out=x_codes[lo][:].bitcast(FP8X4),
                 scales=x_bytes[lo][:],
-                in_=grouped[lo][:].rearrange("p c t -> p (c t)"),
+                in_=grouped[:, lo:hi, :].rearrange("p c t -> p (c t)"),
             )
 
         def products(b, i, pieces, acc):

@@ -1,7 +1,6 @@
 from contextlib import ExitStack
 
 import concourse.mybir as mybir
-from concourse.masks import make_identity
 
 K, T, S, N, U = 512, 1024, 512, 256, 1024
 FLOPS = 2 * 2 * K * N * S
@@ -19,9 +18,10 @@ ALU = mybir.AluOpType
 P = 128
 PACK = 4
 LIST_ROWS = 16
-PIECES = ((0, 128), (128, 256), (256, 512))
 CAND, GATE = 0, 1
+PLANE_ROW = (4, 0)
 HALF = S // 2
+QUARTER = S // 4
 
 
 def tile_picked_gmem_tanh_e_kernel(
@@ -37,167 +37,120 @@ def tile_picked_gmem_tanh_e_kernel(
         x_rows = [keep.tile([P, T], F32, name="x_row%d" % j, align_bytes=64) for j in range(PACK)]
         window = [keep.tile([P, U], F32, name="window%d" % b) for b in range(2)]
         w_codes = [keep.tile([P, N], U32, name="w_codes%d" % i, align_bytes=64) for i in range(2)]
-        w_bytes = {GATE: keep.tile([P, N], U8, name="gate_bytes", align_bytes=64)}
+        w_bytes = keep.tile([P, N], U8, name="w_bytes", align_bytes=64)
         warm = keep.tile([P, 2], F32, name="warm")
 
         def entries(lst, lo, hi):
             return lst[:, lo // LIST_ROWS : hi // LIST_ROWS]
 
         nc.vector.memset(warm[:, 0:1], 0.0)
-        ident = keep.tile([P, P], F32, name="ident")
-        make_identity(nc, ident[:])
 
         x_view = xT.rearrange("(p j) t -> p j t", j=PACK)
 
         def load_words(i, words):
             nc.sync.dma_start(w_codes[i][:].bitcast(I32), words[0].rearrange("p n t -> p (n t)").bitcast(I32))
 
-        def load_scales(queue, i, scales, q):
-            queue.dma_start(
-                w_bytes[i][32 * q : 32 * q + 4, :].bitcast(I32), scales[0, 4 * q : 4 * q + 4, :].bitcast(I32)
-            )
+        def load_scales(queue, i, scales, quadrants):
+            for q in quadrants:
+                first = 32 * q + PLANE_ROW[i]
+                queue.dma_start(
+                    w_bytes[first : first + 4, :].bitcast(I32), scales[0, 4 * q : 4 * q + 4, :].bitcast(I32)
+                )
 
         nc.sync.dma_start(x_rows[0][:], x_view[:, 0, :])
         nc.sync.dma_start(offs_sb[:], offs)
         nc.sync.dma_start(x_rows[1][:], x_view[:, 1, :])
         nc.sync.dma_start(x_rows[2][:], x_view[:, 2, :])
         nc.sync.dma_start(x_rows[3][:], x_view[:, 3, :])
-        nc.sync.dma_start(slot_sb[:], slot)
-        nc.sync.dma_start(window[0][:], mem[0:P, :])
+        load_scales(nc.sync, CAND, w1_scales, range(0, 2))
         load_words(GATE, w2_words)
-        nc.sync.dma_start(window[1][:], mem[P : 2 * P, :])
         load_words(CAND, w1_words)
-        load_scales(nc.scalar, GATE, w2_scales, 0)
-        load_scales(nc.scalar, GATE, w2_scales, 1)
-        load_scales(nc.scalar, GATE, w2_scales, 2)
-        load_scales(nc.scalar, GATE, w2_scales, 3)
+        load_scales(nc.sync, CAND, w1_scales, range(2, 4))
+        nc.sync.dma_start(window[0][:], mem[0:P, :])
+        nc.sync.dma_start(slot_sb[:], slot)
+        nc.sync.dma_start(window[1][:], mem[P : 2 * P, :])
+        load_scales(nc.scalar, GATE, w2_scales, range(4))
         nc.scalar.activation(warm[:, 1:2], warm[:, 0:1], ACT.Sigmoid)
 
-        PAD = 2 * S - 256
-        shared = keep.tile([P, PAD + 2 * S], BF16, name="shared")
-        picked = shared[:, PAD : PAD + 2 * S].rearrange("p (t s) -> p t s", t=2)
-        old = shared[:, 0 : 2 * S].bitcast(F32)
-        grouped = keep.tile([P, S, PACK], BF16, name="grouped", align_bytes=64)
-        for j in range(2):
-            rounded = keep.tile([P, T], BF16, name="rounded%d" % j)
-            nc.vector.tensor_copy(rounded[:], x_rows[j][:])
-            nc.scalar.activation(grouped[:, :, j], rounded[:].indirect(offs_sb[:]), ACT.Copy)
-        nc.vector.tensor_copy(picked[:, 0, :], x_rows[2][:].indirect(offs_sb[:]))
-        w_bytes[CAND] = keep.tile([P, N], U8, name="x_row1", align_bytes=64)
-        for q in range(4):
-            load_scales(nc.scalar, CAND, w1_scales, q)
-        for lo, hi in PIECES:
-            nc.vector.tensor_copy(picked[:, 1, lo:hi], x_rows[PACK - 1][:].indirect(entries(offs_sb, lo, hi)))
+        grouped = [keep.tile([P, HALF, PACK], BF16, name="grouped%d" % h, align_bytes=64) for h in range(2)]
+        picked = keep.tile([P, PACK, HALF], BF16, name="picked")
+        x_codes = keep.tile([P, S], U32, name="x_codes", align_bytes=64)
+        x_bytes = keep.tile([P, S], U8, name="x_bytes", align_bytes=64)
 
-        x_codes = {lo: keep.tile([P, hi - lo], U32, name="x_codes%d" % lo, align_bytes=64) for lo, hi in PIECES}
-        x_bytes = {lo: keep.tile([P, hi - lo], U8, name="x_bytes%d" % lo, align_bytes=64) for lo, hi in PIECES}
-        keep_gate = keep.tile([P, S], F32, name="keep_gate")
-        neg_cand = keep.tile([P, S], F32, name="neg_cand")
-        kept = keep.tile([P, S], F32, name="kept")
-        added = keep.tile([P, S], F32, name="added")
-        gate = keep.tile([P, S], F32, name="gate")
-        cand_t = keep.tile([P, S], F32, name="cand_t")
-        neg_old_t = keep.tile([P, S], F32, name="neg_old_t")
-        pull = keep.tile([P, S], F32, name="pull")
-        old1 = keep.tile([P, HALF], F32, name="old1")
+        def pair(j):
+            nc.scalar.copy(grouped[1][:, :, j : j + 2], picked[:, j : j + 2, :].rearrange("p t s -> p s t"))
 
-        def interleave(lo, hi):
-            nc.scalar.copy(
-                grouped[:, lo:hi, 2:PACK],
-                picked[:, :, lo:hi].rearrange("p t s -> p s t"),
-            )
-
-        def quantise(lo, hi):
+        def quantise(h, lo, hi):
             nc.vector.quantize_mx(
-                out=x_codes[lo][:].bitcast(FP8X4),
-                scales=x_bytes[lo][:],
-                in_=grouped[:, lo:hi, :].rearrange("p c t -> p (c t)"),
+                out=x_codes[:, h * HALF + lo : h * HALF + hi].bitcast(FP8X4),
+                scales=x_bytes[:, h * HALF + lo : h * HALF + hi],
+                in_=grouped[h][:, lo:hi, :].rearrange("p c t -> p (c t)"),
             )
 
-        def products(b, i, pieces, acc):
-            first = pieces[0][0]
+        for j in range(PACK):
+            pieces = ((0, QUARTER), (QUARTER, HALF)) if j == PACK - 1 else ((0, HALF),)
             for lo, hi in pieces:
-                nc.tensor.matmul_mx(
-                    out=acc[:, lo - first : hi - first],
-                    lhsT=w_codes[i][:, b * P : (b + 1) * P].bitcast(FP8X4),
-                    lhsT_scale=w_bytes[i][:, b * P : (b + 1) * P],
-                    rhs=x_codes[lo][:].bitcast(FP8X4),
-                    rhs_scale=x_bytes[lo][:],
-                    start=True,
-                    stop=True,
-                )
+                nc.vector.tensor_copy(grouped[0][:, lo:hi, j], x_rows[j][:].indirect(entries(offs_sb, lo, hi)))
+            nc.scalar.activation(picked[:, j, :], x_rows[j][:].indirect(entries(offs_sb, HALF, S)), ACT.Copy)
+            if j % 2 == 1:
+                pair(j - 1)
+        quantise(0, 0, QUARTER)
+        quantise(0, QUARTER, HALF)
+        quantise(1, 0, HALF)
 
-        def bank(name, width):
-            return psum.tile([P, width], F32, name=name)[:]
+        keep_gate = [keep.tile([P, S], F32, name="keep_gate%d" % b) for b in range(2)]
+        neg_cand = [keep.tile([P, S], F32, name="neg_cand%d" % b) for b in range(2)]
+        kept = [keep.tile([P, S], F32, name="kept%d" % b) for b in range(2)]
+        added = [keep.tile([P, S], F32, name="added%d" % b) for b in range(2)]
+        new0 = keep.tile([P, S], F32, name="new0")
 
-        def half(b):
-            return slice(b * HALF, (b + 1) * HALF)
-
-        def put(b, lo, first, second):
-            nc.vector.tensor_tensor(window[b][:].indirect(entries(slot_sb, lo, lo + HALF)), first, second, ALU.add)
-
-        a, bb, c = PIECES
-        for piece in PIECES:
-            interleave(*piece)
-        nc.vector.tensor_copy(old[:, 0:128], window[0][:].indirect(entries(slot_sb, 0, 128)))
-        quantise(*a)
-        quantise(*bb)
-        for i in (GATE, CAND):
-            for b in range(2):
-                acc = bank("first%d_%d" % (i, b), HALF)
-                products(b, i, [a, bb], acc)
-                if i == GATE:
-                    nc.scalar.activation(keep_gate[:, half(b)], acc, ACT.Sigmoid, scale=-1.0)
-                else:
-                    nc.scalar.activation(neg_cand[:, half(b)], acc, ACT.Tanh, scale=-1.0)
-        nc.vector.tensor_copy(old[:, 128:512], window[0][:].indirect(entries(slot_sb, 128, 512)))
-        quantise(*c)
-        nc.vector.tensor_copy(old1[:], window[1][:].indirect(entries(slot_sb, HALF, S)))
-        nc.vector.tensor_tensor(kept[:, half(0)], old[:, 0:HALF], keep_gate[:, half(0)], ALU.mult)
-        nc.vector.tensor_tensor(
-            kept[:, half(1)], window[1][:].indirect(entries(slot_sb, 0, HALF)), keep_gate[:, half(1)], ALU.mult
-        )
-        for b in range(2):
-            nc.vector.scalar_tensor_tensor(
-                added[:, half(b)], keep_gate[:, half(b)], 1.0, neg_cand[:, half(b)], ALU.subtract, ALU.mult
-            )
-        late_old = [old[:, HALF:S], old1[:]]
-
-        turned = bank("turned", S)
-        for t in range(2):
-            cols = slice(t * P, (t + 1) * P)
+        def product(b, i, lo, hi, name):
+            acc = psum.tile([P, hi - lo], F32, name=name)
             nc.tensor.matmul_mx(
-                out=turned[:, half(t)],
-                lhsT=x_codes[HALF][:, cols].bitcast(FP8X4),
-                lhsT_scale=x_bytes[HALF][:, cols],
-                rhs=w_codes[CAND][:].bitcast(FP8X4),
-                rhs_scale=w_bytes[CAND][:],
+                out=acc[:],
+                lhsT=w_codes[i][:, b * P : (b + 1) * P].bitcast(FP8X4),
+                lhsT_scale=w_bytes[PLANE_ROW[i] : P, b * P : (b + 1) * P],
+                rhs=x_codes[:, lo:hi].bitcast(FP8X4),
+                rhs_scale=x_bytes[:, lo:hi],
                 start=True,
                 stop=True,
             )
-        nc.scalar.activation(cand_t[:], turned, ACT.Tanh)
-        acc = bank("first%d_0" % CAND, S)
-        for b in range(2):
-            products(b, GATE, [c], acc[:, half(b)])
-        nc.scalar.activation(gate[:], acc, ACT.Sigmoid)
-        old_t = bank("first%d_1" % CAND, S)
-        for b in range(2):
-            for t in range(2):
-                at = t * HALF + b * P
-                nc.tensor.transpose(old_t[:, at : at + P], late_old[b][:, t * P : (t + 1) * P], ident[:])
-        nc.scalar.activation(neg_old_t[:], old_t, ACT.Copy, scale=-1.0)
-        diff = bank("diff", S)
-        for b in range(2):
-            for t in range(2):
-                src = slice(t * HALF + b * P, t * HALF + (b + 1) * P)
-                dst = slice(b * HALF + t * P, b * HALF + (t + 1) * P)
-                nc.tensor.matmul(diff[:, dst], neg_old_t[:, src], ident[:], start=True, stop=False, is_transpose=True)
-                nc.tensor.matmul(diff[:, dst], cand_t[:, src], ident[:], start=False, stop=True, is_transpose=True)
+            if i == GATE:
+                nc.scalar.activation(keep_gate[b][:, lo:hi], acc[:], ACT.Sigmoid, scale=-1.0)
+            else:
+                nc.scalar.activation(neg_cand[b][:, lo:hi], acc[:], ACT.Tanh, scale=-1.0)
 
-        put(0, 0, kept[:, half(0)], added[:, half(0)])
-        put(1, 0, kept[:, half(1)], added[:, half(1)])
-        for b in range(2):
-            nc.vector.tensor_tensor(pull[:, half(b)], diff[:, half(b)], gate[:, half(b)], ALU.mult)
-        for b in range(2):
-            put(b, HALF, pull[:, half(b)], late_old[b])
-            nc.sync.dma_start(out[b * P : (b + 1) * P, :], window[b][:])
+        def old_part(b, lo, hi):
+            nc.vector.tensor_tensor(
+                kept[b][:, lo:hi], window[b][:].indirect(entries(slot_sb, lo, hi)), keep_gate[b][:, lo:hi], ALU.mult
+            )
+
+        def new_part(b, lo, hi):
+            nc.vector.scalar_tensor_tensor(
+                added[b][:, lo:hi], keep_gate[b][:, lo:hi], 1.0, neg_cand[b][:, lo:hi], ALU.subtract, ALU.mult
+            )
+
+        def join0(lo, hi):
+            nc.vector.tensor_tensor(new0[:, lo:hi], kept[0][:, lo:hi], added[0][:, lo:hi], ALU.add)
+
+        def put0(lo, hi):
+            nc.scalar.activation(window[0][:].indirect(entries(slot_sb, lo, hi)), new0[:, lo:hi], ACT.Copy)
+
+        for lo in (0, HALF):
+            for b in range(2):
+                for i in (GATE, CAND):
+                    product(b, i, lo, lo + HALF, "acc%d_%d_%d" % (lo, b, i))
+
+        old_part(0, 0, HALF)
+        new_part(0, 0, HALF)
+        old_part(0, HALF, S)
+        join0(0, HALF)
+        new_part(0, HALF, S)
+        put0(0, HALF)
+        old_part(1, 0, S)
+        new_part(1, 0, S)
+        join0(HALF, S)
+        put0(HALF, S)
+        nc.sync.dma_start(out[0:P, :], window[0][:])
+        nc.vector.tensor_tensor(window[1][:].indirect(slot_sb[:]), kept[1][:], added[1][:], ALU.add)
+        nc.sync.dma_start(out[P : 2 * P, :], window[1][:])

@@ -22,6 +22,8 @@ CAND, GATE = 0, 1
 PLANE_ROW = (4, 0)
 HALF = S // 2
 QUARTER = S // 4
+SPLIT = 352
+MID = 448
 
 
 def tile_picked_gmem_tanh_e_kernel(
@@ -50,64 +52,70 @@ def tile_picked_gmem_tanh_e_kernel(
         def load_words(i, words):
             nc.sync.dma_start(w_codes[i][:].bitcast(I32), words[0].rearrange("p n t -> p (n t)").bitcast(I32))
 
-        def load_scales(queue, i, scales, quadrants):
+        def load_scales(i, scales, quadrants):
             for q in quadrants:
                 first = 32 * q + PLANE_ROW[i]
-                queue.dma_start(
+                nc.sync.dma_start(
                     w_bytes[first : first + 4, :].bitcast(I32), scales[0, 4 * q : 4 * q + 4, :].bitcast(I32)
                 )
 
         nc.sync.dma_start(x_rows[0][:], x_view[:, 0, :])
         nc.sync.dma_start(offs_sb[:], offs)
-        nc.sync.dma_start(x_rows[1][:], x_view[:, 1, :])
-        nc.sync.dma_start(x_rows[2][:], x_view[:, 2, :])
-        nc.sync.dma_start(x_rows[3][:], x_view[:, 3, :])
-        load_scales(nc.sync, CAND, w1_scales, range(0, 2))
+        load_scales(GATE, w2_scales, range(4))
+        for j in range(1, PACK):
+            nc.sync.dma_start(x_rows[j][:], x_view[:, j, :])
+        load_scales(CAND, w1_scales, range(3))
         load_words(GATE, w2_words)
         load_words(CAND, w1_words)
-        load_scales(nc.sync, CAND, w1_scales, range(2, 4))
+        load_scales(CAND, w1_scales, range(3, 4))
         nc.sync.dma_start(window[0][:], mem[0:P, :])
         nc.sync.dma_start(slot_sb[:], slot)
         nc.sync.dma_start(window[1][:], mem[P : 2 * P, :])
-        load_scales(nc.scalar, GATE, w2_scales, range(4))
         nc.scalar.activation(warm[:, 1:2], warm[:, 0:1], ACT.Sigmoid)
 
-        grouped = [keep.tile([P, HALF, PACK], BF16, name="grouped%d" % h, align_bytes=64) for h in range(2)]
-        picked = keep.tile([P, PACK, HALF], BF16, name="picked")
+        grouped = keep.tile([P, S, PACK], BF16, name="grouped", align_bytes=64)
+        picked = keep.tile([P, PACK, S - SPLIT], BF16, name="picked")
         x_codes = keep.tile([P, S], U32, name="x_codes", align_bytes=64)
         x_bytes = keep.tile([P, S], U8, name="x_bytes", align_bytes=64)
 
-        def pair(j):
-            nc.scalar.copy(grouped[1][:, :, j : j + 2], picked[:, j : j + 2, :].rearrange("p t s -> p s t"))
+        def pair(j, lo, hi):
+            nc.scalar.copy(
+                grouped[:, lo:hi, j : j + 2], picked[:, j : j + 2, lo - SPLIT : hi - SPLIT].rearrange("p t s -> p s t")
+            )
 
-        def quantise(h, lo, hi):
+        def quantise(lo, hi):
             nc.vector.quantize_mx(
-                out=x_codes[:, h * HALF + lo : h * HALF + hi].bitcast(FP8X4),
-                scales=x_bytes[:, h * HALF + lo : h * HALF + hi],
-                in_=grouped[h][:, lo:hi, :].rearrange("p c t -> p (c t)"),
+                out=x_codes[:, lo:hi].bitcast(FP8X4),
+                scales=x_bytes[:, lo:hi],
+                in_=grouped[:, lo:hi, :].rearrange("p c t -> p (c t)"),
             )
 
         for j in range(PACK):
-            pieces = ((0, QUARTER), (QUARTER, HALF)) if j == PACK - 1 else ((0, HALF),)
+            pieces = ((0, QUARTER), (QUARTER, SPLIT)) if j == PACK - 1 else ((0, SPLIT),)
             for lo, hi in pieces:
-                nc.vector.tensor_copy(grouped[0][:, lo:hi, j], x_rows[j][:].indirect(entries(offs_sb, lo, hi)))
-            nc.scalar.activation(picked[:, j, :], x_rows[j][:].indirect(entries(offs_sb, HALF, S)), ACT.Copy)
+                nc.vector.tensor_copy(grouped[:, lo:hi, j], x_rows[j][:].indirect(entries(offs_sb, lo, hi)))
+            pieces = ((SPLIT, MID), (MID, S)) if j == PACK - 1 else ((SPLIT, S),)
+            for lo, hi in pieces:
+                nc.scalar.activation(
+                    picked[:, j, lo - SPLIT : hi - SPLIT], x_rows[j][:].indirect(entries(offs_sb, lo, hi)), ACT.Copy
+                )
             if j % 2 == 1:
-                pair(j - 1)
-        quantise(0, 0, QUARTER)
-        quantise(0, QUARTER, HALF)
-        quantise(1, 0, HALF)
+                for lo, hi in pieces:
+                    pair(j - 1, lo, hi)
+        quantise(0, QUARTER)
+        quantise(QUARTER, HALF)
+        quantise(HALF, S)
 
         keep_gate = [keep.tile([P, S], F32, name="keep_gate%d" % b) for b in range(2)]
         neg_cand = [keep.tile([P, S], F32, name="neg_cand%d" % b) for b in range(2)]
         kept = [keep.tile([P, S], F32, name="kept%d" % b) for b in range(2)]
-        added = [keep.tile([P, S], F32, name="added%d" % b) for b in range(2)]
-        new0 = keep.tile([P, S], F32, name="new0")
+        added = [keep_gate[0], keep.tile([P, S], F32, name="added1")]
+        new0 = keep.tile([P, HALF], F32, name="new0")
+        old1 = keep.tile([P, HALF], F32, name="old1")
 
-        def product(b, i, lo, hi, name):
-            acc = psum.tile([P, hi - lo], F32, name=name)
+        def product(b, i, lo, hi, acc):
             nc.tensor.matmul_mx(
-                out=acc[:],
+                out=acc,
                 lhsT=w_codes[i][:, b * P : (b + 1) * P].bitcast(FP8X4),
                 lhsT_scale=w_bytes[PLANE_ROW[i] : P, b * P : (b + 1) * P],
                 rhs=x_codes[:, lo:hi].bitcast(FP8X4),
@@ -115,10 +123,24 @@ def tile_picked_gmem_tanh_e_kernel(
                 start=True,
                 stop=True,
             )
+
+        def activate(b, i, lo, hi, acc):
             if i == GATE:
-                nc.scalar.activation(keep_gate[b][:, lo:hi], acc[:], ACT.Sigmoid, scale=-1.0)
+                nc.scalar.activation(keep_gate[b][:, lo:hi], acc, ACT.Sigmoid, scale=-1.0)
             else:
-                nc.scalar.activation(neg_cand[b][:, lo:hi], acc[:], ACT.Tanh, scale=-1.0)
+                nc.scalar.activation(neg_cand[b][:, lo:hi], acc, ACT.Tanh, scale=-1.0)
+
+        def bank(name, *parts):
+            acc = psum.tile([P, S], F32, name=name)
+            at = 0
+            places = []
+            for b, i, lo, hi in parts:
+                places.append(acc[:, at : at + hi - lo])
+                at += hi - lo
+            for part, place in zip(parts, places):
+                product(*part, place)
+            for part, place in zip(parts, places):
+                activate(*part, place)
 
         def old_part(b, lo, hi):
             nc.vector.tensor_tensor(
@@ -130,27 +152,40 @@ def tile_picked_gmem_tanh_e_kernel(
                 added[b][:, lo:hi], keep_gate[b][:, lo:hi], 1.0, neg_cand[b][:, lo:hi], ALU.subtract, ALU.mult
             )
 
-        def join0(lo, hi):
-            nc.vector.tensor_tensor(new0[:, lo:hi], kept[0][:, lo:hi], added[0][:, lo:hi], ALU.add)
+        def join0(dst, lo):
+            nc.vector.tensor_tensor(dst, kept[0][:, lo : lo + HALF], added[0][:, lo : lo + HALF], ALU.add)
 
-        def put0(lo, hi):
-            nc.scalar.activation(window[0][:].indirect(entries(slot_sb, lo, hi)), new0[:, lo:hi], ACT.Copy)
+        def put0(src, lo):
+            nc.scalar.activation(window[0][:].indirect(entries(slot_sb, lo, lo + HALF)), src, ACT.Copy)
 
-        for lo in (0, HALF):
-            for b in range(2):
-                for i in (GATE, CAND):
-                    product(b, i, lo, lo + HALF, "acc%d_%d_%d" % (lo, b, i))
+        for n, part in enumerate(
+            (
+                (0, GATE, 0, QUARTER),
+                (0, GATE, QUARTER, HALF),
+                (0, CAND, 0, HALF),
+                (0, GATE, HALF, S),
+                (0, CAND, HALF, S),
+                (1, GATE, 0, HALF),
+                (1, CAND, 0, S),
+                (1, GATE, HALF, S),
+            )
+        ):
+            bank("acc%d" % n, part)
 
-        old_part(0, 0, HALF)
-        new_part(0, 0, HALF)
+        nc.scalar.activation(old1[:], window[1][:].indirect(entries(slot_sb, HALF, S)), ACT.Copy)
+        old_part(0, 0, QUARTER)
+        old_part(0, QUARTER, HALF)
+        new_part(0, 0, QUARTER)
+        new_part(0, QUARTER, HALF)
         old_part(0, HALF, S)
-        join0(0, HALF)
+        join0(new0[:], 0)
+        put0(new0[:], 0)
         new_part(0, HALF, S)
-        put0(0, HALF)
-        old_part(1, 0, S)
+        old_part(1, 0, HALF)
         new_part(1, 0, S)
-        join0(HALF, S)
-        put0(HALF, S)
+        nc.vector.tensor_tensor(kept[1][:, HALF:S], old1[:], keep_gate[1][:, HALF:S], ALU.mult)
+        join0(neg_cand[1][:, HALF:S], HALF)
+        put0(neg_cand[1][:, HALF:S], HALF)
         nc.sync.dma_start(out[0:P, :], window[0][:])
         nc.vector.tensor_tensor(window[1][:].indirect(slot_sb[:]), kept[1][:], added[1][:], ALU.add)
         nc.sync.dma_start(out[P : 2 * P, :], window[1][:])

@@ -22,8 +22,8 @@ CAND, GATE = 0, 1
 PLANE_ROW = (4, 0)
 HALF = S // 2
 QUARTER = S // 4
-SPLIT = 352
-MID = 448
+SPLIT = 320
+MID = 416
 
 
 def tile_picked_gmem_tanh_e_kernel(
@@ -52,25 +52,25 @@ def tile_picked_gmem_tanh_e_kernel(
         def load_words(i, words):
             nc.sync.dma_start(w_codes[i][:].bitcast(I32), words[0].rearrange("p n t -> p (n t)").bitcast(I32))
 
-        def load_scales(i, scales, quadrants):
+        def load_scales(queue, i, scales, quadrants):
             for q in quadrants:
                 first = 32 * q + PLANE_ROW[i]
-                nc.sync.dma_start(
+                queue.dma_start(
                     w_bytes[first : first + 4, :].bitcast(I32), scales[0, 4 * q : 4 * q + 4, :].bitcast(I32)
                 )
 
         nc.sync.dma_start(x_rows[0][:], x_view[:, 0, :])
         nc.sync.dma_start(offs_sb[:], offs)
-        load_scales(GATE, w2_scales, range(4))
         for j in range(1, PACK):
             nc.sync.dma_start(x_rows[j][:], x_view[:, j, :])
-        load_scales(CAND, w1_scales, range(3))
+        load_scales(nc.sync, CAND, w1_scales, range(2))
         load_words(GATE, w2_words)
         load_words(CAND, w1_words)
-        load_scales(CAND, w1_scales, range(3, 4))
+        load_scales(nc.sync, CAND, w1_scales, range(2, 4))
         nc.sync.dma_start(window[0][:], mem[0:P, :])
         nc.sync.dma_start(slot_sb[:], slot)
         nc.sync.dma_start(window[1][:], mem[P : 2 * P, :])
+        load_scales(nc.scalar, GATE, w2_scales, range(4))
         nc.scalar.activation(warm[:, 1:2], warm[:, 0:1], ACT.Sigmoid)
 
         grouped = keep.tile([P, S, PACK], BF16, name="grouped", align_bytes=64)

@@ -18,11 +18,12 @@ ALU = mybir.AluOpType
 P = 128
 PACK = 4
 LIST_ROWS = 16
+BANKS = 8
 CAND, GATE = 0, 1
 PLANE_ROW = (4, 0)
 HALF = S // 2
 QUARTER = S // 4
-SPLIT = 320
+SPLIT = (256, 320)
 MID = 416
 
 
@@ -74,13 +75,14 @@ def tile_picked_gmem_tanh_e_kernel(
         nc.scalar.activation(warm[:, 1:2], warm[:, 0:1], ACT.Sigmoid)
 
         grouped = keep.tile([P, S, PACK], BF16, name="grouped", align_bytes=64)
-        picked = keep.tile([P, PACK, S - SPLIT], BF16, name="picked")
+        picked = [keep.tile([P, 2, S - SPLIT[u]], BF16, name="picked%d" % u) for u in range(2)]
         x_codes = keep.tile([P, S], U32, name="x_codes", align_bytes=64)
         x_bytes = keep.tile([P, S], U8, name="x_bytes", align_bytes=64)
 
-        def pair(j, lo, hi):
+        def pair(u, lo, hi):
             nc.scalar.copy(
-                grouped[:, lo:hi, j : j + 2], picked[:, j : j + 2, lo - SPLIT : hi - SPLIT].rearrange("p t s -> p s t")
+                grouped[:, lo:hi, 2 * u : 2 * u + 2],
+                picked[u][:, :, lo - SPLIT[u] : hi - SPLIT[u]].rearrange("p t s -> p s t"),
             )
 
         def quantise(lo, hi):
@@ -91,17 +93,21 @@ def tile_picked_gmem_tanh_e_kernel(
             )
 
         for j in range(PACK):
-            pieces = ((0, QUARTER), (QUARTER, SPLIT)) if j == PACK - 1 else ((0, SPLIT),)
+            u = j // 2
+            split = SPLIT[u]
+            pieces = ((0, QUARTER), (QUARTER, split)) if j == PACK - 1 else ((0, split),)
             for lo, hi in pieces:
                 nc.vector.tensor_copy(grouped[:, lo:hi, j], x_rows[j][:].indirect(entries(offs_sb, lo, hi)))
-            pieces = ((SPLIT, MID), (MID, S)) if j == PACK - 1 else ((SPLIT, S),)
+            pieces = ((split, MID), (MID, S)) if j == PACK - 1 else ((split, S),)
             for lo, hi in pieces:
                 nc.scalar.activation(
-                    picked[:, j, lo - SPLIT : hi - SPLIT], x_rows[j][:].indirect(entries(offs_sb, lo, hi)), ACT.Copy
+                    picked[u][:, j % 2, lo - split : hi - split],
+                    x_rows[j][:].indirect(entries(offs_sb, lo, hi)),
+                    ACT.Copy,
                 )
             if j % 2 == 1:
                 for lo, hi in pieces:
-                    pair(j - 1, lo, hi)
+                    pair(u, lo, hi)
         quantise(0, QUARTER)
         quantise(QUARTER, HALF)
         quantise(HALF, S)
@@ -166,11 +172,12 @@ def tile_picked_gmem_tanh_e_kernel(
                 (0, GATE, HALF, S),
                 (0, CAND, HALF, S),
                 (1, GATE, 0, HALF),
-                (1, CAND, 0, S),
+                (1, CAND, 0, HALF),
+                (1, CAND, HALF, S),
                 (1, GATE, HALF, S),
             )
         ):
-            bank("acc%d" % n, part)
+            bank("acc%d" % (n % BANKS), part)
 
         nc.scalar.activation(old1[:], window[1][:].indirect(entries(slot_sb, HALF, S)), ACT.Copy)
         old_part(0, 0, QUARTER)

@@ -18,7 +18,6 @@ ALU = mybir.AluOpType
 P = 128
 PACK = 4
 LIST_ROWS = 16
-BANKS = 8
 CAND, GATE = 0, 1
 PLANE_ROW = (4, 0)
 HALF = S // 2
@@ -64,13 +63,14 @@ def tile_picked_gmem_tanh_e_kernel(
         nc.sync.dma_start(offs_sb[:], offs)
         for j in range(1, PACK):
             nc.sync.dma_start(x_rows[j][:], x_view[:, j, :])
-        load_scales(nc.sync, CAND, w1_scales, range(2))
+        nc.sync.dma_start(slot_sb[:], slot)
+        load_scales(nc.sync, CAND, w1_scales, range(1))
         load_words(GATE, w2_words)
         load_words(CAND, w1_words)
-        load_scales(nc.sync, CAND, w1_scales, range(2, 4))
+        load_scales(nc.sync, CAND, w1_scales, range(1, 2))
         nc.sync.dma_start(window[0][:], mem[0:P, :])
-        nc.sync.dma_start(slot_sb[:], slot)
         nc.sync.dma_start(window[1][:], mem[P : 2 * P, :])
+        load_scales(nc.gpsimd, CAND, w1_scales, range(2, 4))
         load_scales(nc.scalar, GATE, w2_scales, range(4))
         nc.scalar.activation(warm[:, 1:2], warm[:, 0:1], ACT.Sigmoid)
 
@@ -117,6 +117,7 @@ def tile_picked_gmem_tanh_e_kernel(
         kept = [keep.tile([P, S], F32, name="kept%d" % b) for b in range(2)]
         added = [keep_gate[0], keep.tile([P, S], F32, name="added1")]
         new0 = keep.tile([P, HALF], F32, name="new0")
+        old0 = keep.tile([P, HALF], F32, name="old0")
         old1 = keep.tile([P, HALF], F32, name="old1")
 
         def product(b, i, lo, hi, acc):
@@ -136,17 +137,7 @@ def tile_picked_gmem_tanh_e_kernel(
             else:
                 nc.scalar.activation(neg_cand[b][:, lo:hi], acc, ACT.Tanh, scale=-1.0)
 
-        def bank(name, *parts):
-            acc = psum.tile([P, S], F32, name=name)
-            at = 0
-            places = []
-            for b, i, lo, hi in parts:
-                places.append(acc[:, at : at + hi - lo])
-                at += hi - lo
-            for part, place in zip(parts, places):
-                product(*part, place)
-            for part, place in zip(parts, places):
-                activate(*part, place)
+        acc = [psum.tile([P, HALF], F32, name="acc%d" % n) for n in range(8)]
 
         def old_part(b, lo, hi):
             nc.vector.tensor_tensor(
@@ -164,27 +155,21 @@ def tile_picked_gmem_tanh_e_kernel(
         def put0(src, lo):
             nc.scalar.activation(window[0][:].indirect(entries(slot_sb, lo, lo + HALF)), src, ACT.Copy)
 
-        for n, part in enumerate(
-            (
-                (0, GATE, 0, QUARTER),
-                (0, GATE, QUARTER, HALF),
-                (0, CAND, 0, HALF),
-                (0, GATE, HALF, S),
-                (0, CAND, HALF, S),
-                (1, GATE, 0, HALF),
-                (1, CAND, 0, HALF),
-                (1, CAND, HALF, S),
-                (1, GATE, HALF, S),
-            )
-        ):
-            bank("acc%d" % (n % BANKS), part)
+        for lo in (0, QUARTER):
+            for n, i in enumerate((GATE, CAND)):
+                product(0, i, lo, lo + QUARTER, acc[n][:, lo : lo + QUARTER])
+        for n, i in enumerate((GATE, CAND)):
+            activate(0, i, 0, HALF, acc[n][:])
+        later = ((1, GATE, 0), (0, GATE, HALF), (0, CAND, HALF), (1, CAND, 0), (1, CAND, HALF), (1, GATE, HALF))
+        for n, (b, i, lo) in enumerate(later):
+            product(b, i, lo, lo + HALF, acc[2 + n][:])
+            activate(b, i, lo, lo + HALF, acc[2 + n][:])
 
         nc.scalar.activation(old1[:], window[1][:].indirect(entries(slot_sb, HALF, S)), ACT.Copy)
-        old_part(0, 0, QUARTER)
-        old_part(0, QUARTER, HALF)
-        new_part(0, 0, QUARTER)
-        new_part(0, QUARTER, HALF)
-        old_part(0, HALF, S)
+        nc.vector.tensor_copy(old0[:], window[0][:].indirect(entries(slot_sb, HALF, S)))
+        old_part(0, 0, HALF)
+        nc.vector.tensor_tensor(kept[0][:, HALF:S], old0[:], keep_gate[0][:, HALF:S], ALU.mult)
+        new_part(0, 0, HALF)
         join0(new0[:], 0)
         put0(new0[:], 0)
         new_part(0, HALF, S)

@@ -19,7 +19,6 @@ P = 128
 PACK = 4
 LIST_ROWS = 16
 CAND, GATE = 0, 1
-PLANE_ROW = (4, 0)
 HALF = S // 2
 QUARTER = S // 4
 SPLIT = (256, 320)
@@ -39,7 +38,7 @@ def tile_picked_gmem_tanh_e_kernel(
         x_rows = [keep.tile([P, T], F32, name="x_row%d" % j, align_bytes=64) for j in range(PACK)]
         window = [keep.tile([P, U], F32, name="window%d" % b) for b in range(2)]
         w_codes = [keep.tile([P, N], U32, name="w_codes%d" % i, align_bytes=64) for i in range(2)]
-        w_bytes = keep.tile([P, N], U8, name="w_bytes", align_bytes=64)
+        w_bytes = [keep.tile([P, N], U8, name="w_bytes%d" % i, align_bytes=64) for i in range(2)]
         warm = keep.tile([P, 2], F32, name="warm")
 
         def entries(lst, lo, hi):
@@ -54,9 +53,8 @@ def tile_picked_gmem_tanh_e_kernel(
 
         def load_scales(queue, i, scales, quadrants):
             for q in quadrants:
-                first = 32 * q + PLANE_ROW[i]
                 queue.dma_start(
-                    w_bytes[first : first + 4, :].bitcast(I32), scales[0, 4 * q : 4 * q + 4, :].bitcast(I32)
+                    w_bytes[i][32 * q : 32 * q + 4, :].bitcast(I32), scales[0, 4 * q : 4 * q + 4, :].bitcast(I32)
                 )
 
         nc.sync.dma_start(x_rows[0][:], x_view[:, 0, :])
@@ -64,13 +62,12 @@ def tile_picked_gmem_tanh_e_kernel(
         for j in range(1, PACK):
             nc.sync.dma_start(x_rows[j][:], x_view[:, j, :])
         nc.sync.dma_start(slot_sb[:], slot)
-        load_scales(nc.sync, CAND, w1_scales, range(1))
         load_words(GATE, w2_words)
-        load_words(CAND, w1_words)
-        load_scales(nc.sync, CAND, w1_scales, range(1, 2))
         nc.sync.dma_start(window[0][:], mem[0:P, :])
+        load_scales(nc.sync, CAND, w1_scales, range(3))
+        load_words(CAND, w1_words)
+        load_scales(nc.sync, CAND, w1_scales, range(3, 4))
         nc.sync.dma_start(window[1][:], mem[P : 2 * P, :])
-        load_scales(nc.gpsimd, CAND, w1_scales, range(2, 4))
         load_scales(nc.scalar, GATE, w2_scales, range(4))
         nc.scalar.activation(warm[:, 1:2], warm[:, 0:1], ACT.Sigmoid)
 
@@ -115,16 +112,16 @@ def tile_picked_gmem_tanh_e_kernel(
         keep_gate = [keep.tile([P, S], F32, name="keep_gate%d" % b) for b in range(2)]
         neg_cand = [keep.tile([P, S], F32, name="neg_cand%d" % b) for b in range(2)]
         kept = [keep.tile([P, S], F32, name="kept%d" % b) for b in range(2)]
-        added = [keep_gate[0], keep.tile([P, S], F32, name="added1")]
+        added = [keep.tile([P, S], F32, name="added%d" % b) for b in range(2)]
         new0 = keep.tile([P, HALF], F32, name="new0")
         old0 = keep.tile([P, HALF], F32, name="old0")
-        old1 = keep.tile([P, HALF], F32, name="old1")
+        old1 = keep.tile([P, QUARTER], F32, name="old1")
 
         def product(b, i, lo, hi, acc):
             nc.tensor.matmul_mx(
                 out=acc,
                 lhsT=w_codes[i][:, b * P : (b + 1) * P].bitcast(FP8X4),
-                lhsT_scale=w_bytes[PLANE_ROW[i] : P, b * P : (b + 1) * P],
+                lhsT_scale=w_bytes[i][:, b * P : (b + 1) * P],
                 rhs=x_codes[:, lo:hi].bitcast(FP8X4),
                 rhs_scale=x_bytes[:, lo:hi],
                 start=True,
@@ -137,7 +134,6 @@ def tile_picked_gmem_tanh_e_kernel(
             else:
                 nc.scalar.activation(neg_cand[b][:, lo:hi], acc, ACT.Tanh, scale=-1.0)
 
-        acc = [psum.tile([P, HALF], F32, name="acc%d" % n) for n in range(8)]
 
         def old_part(b, lo, hi):
             nc.vector.tensor_tensor(
@@ -155,29 +151,34 @@ def tile_picked_gmem_tanh_e_kernel(
         def put0(src, lo):
             nc.scalar.activation(window[0][:].indirect(entries(slot_sb, lo, lo + HALF)), src, ACT.Copy)
 
-        for lo in (0, QUARTER):
-            for n, i in enumerate((GATE, CAND)):
-                product(0, i, lo, lo + QUARTER, acc[n][:, lo : lo + QUARTER])
-        for n, i in enumerate((GATE, CAND)):
-            activate(0, i, 0, HALF, acc[n][:])
-        later = ((1, GATE, 0), (0, GATE, HALF), (0, CAND, HALF), (1, CAND, 0), (1, CAND, HALF), (1, GATE, HALF))
-        for n, (b, i, lo) in enumerate(later):
-            product(b, i, lo, lo + HALF, acc[2 + n][:])
-            activate(b, i, lo, lo + HALF, acc[2 + n][:])
+        for name, b, i, lo in (
+            ("gate0a", 0, GATE, 0),
+            ("gate1a", 1, GATE, 0),
+            ("gate0b", 0, GATE, HALF),
+            ("cand0a", 0, CAND, 0),
+            ("cand0b", 0, CAND, HALF),
+            ("cand1a", 1, CAND, 0),
+            ("cand1b", 1, CAND, HALF),
+            ("cand0a", 1, GATE, HALF),
+        ):
+            acc = psum.tile([P, HALF], F32, name=name)
+            product(b, i, lo, lo + HALF, acc[:])
+            activate(b, i, lo, lo + HALF, acc[:])
 
-        nc.scalar.activation(old1[:], window[1][:].indirect(entries(slot_sb, HALF, S)), ACT.Copy)
+        nc.scalar.activation(old1[:], window[1][:].indirect(entries(slot_sb, S - QUARTER, S)), ACT.Copy)
         nc.vector.tensor_copy(old0[:], window[0][:].indirect(entries(slot_sb, HALF, S)))
         old_part(0, 0, HALF)
         nc.vector.tensor_tensor(kept[0][:, HALF:S], old0[:], keep_gate[0][:, HALF:S], ALU.mult)
         new_part(0, 0, HALF)
+        new_part(0, HALF, S)
         join0(new0[:], 0)
         put0(new0[:], 0)
-        new_part(0, HALF, S)
         old_part(1, 0, HALF)
         new_part(1, 0, S)
-        nc.vector.tensor_tensor(kept[1][:, HALF:S], old1[:], keep_gate[1][:, HALF:S], ALU.mult)
-        join0(neg_cand[1][:, HALF:S], HALF)
-        put0(neg_cand[1][:, HALF:S], HALF)
+        old_part(1, HALF, S - QUARTER)
+        nc.vector.tensor_tensor(kept[1][:, S - QUARTER : S], old1[:], keep_gate[1][:, S - QUARTER : S], ALU.mult)
+        join0(keep_gate[1][:, 0:HALF], HALF)
+        put0(keep_gate[1][:, 0:HALF], HALF)
         nc.sync.dma_start(out[0:P, :], window[0][:])
         nc.vector.tensor_tensor(window[1][:].indirect(slot_sb[:]), kept[1][:], added[1][:], ALU.add)
         nc.sync.dma_start(out[P : 2 * P, :], window[1][:])

@@ -51,8 +51,8 @@ def tile_picked_gmem_tanh_e_kernel(
         def load_words(i, words):
             nc.sync.dma_start(w_codes[i][:].bitcast(I32), words[0].rearrange("p n t -> p (n t)").bitcast(I32))
 
-        def load_scales(queue, i, scales, quadrants):
-            for q in quadrants:
+        def load_scales(queue, i, scales):
+            for q in range(4):
                 queue.dma_start(
                     w_bytes[i][32 * q : 32 * q + 4, :].bitcast(I32), scales[0, 4 * q : 4 * q + 4, :].bitcast(I32)
                 )
@@ -64,11 +64,10 @@ def tile_picked_gmem_tanh_e_kernel(
         nc.sync.dma_start(slot_sb[:], slot)
         load_words(GATE, w2_words)
         nc.sync.dma_start(window[0][:], mem[0:P, :])
-        load_scales(nc.sync, CAND, w1_scales, range(3))
+        load_scales(nc.sync, CAND, w1_scales)
         load_words(CAND, w1_words)
-        load_scales(nc.sync, CAND, w1_scales, range(3, 4))
         nc.sync.dma_start(window[1][:], mem[P : 2 * P, :])
-        load_scales(nc.scalar, GATE, w2_scales, range(4))
+        load_scales(nc.scalar, GATE, w2_scales)
         nc.scalar.activation(warm[:, 1:2], warm[:, 0:1], ACT.Sigmoid)
 
         grouped = keep.tile([P, S, PACK], BF16, name="grouped", align_bytes=64)
@@ -151,23 +150,25 @@ def tile_picked_gmem_tanh_e_kernel(
         def put0(src, lo):
             nc.scalar.activation(window[0][:].indirect(entries(slot_sb, lo, lo + HALF)), src, ACT.Copy)
 
-        for name, b, i, lo in (
-            ("gate0a", 0, GATE, 0),
-            ("gate1a", 1, GATE, 0),
-            ("gate0b", 0, GATE, HALF),
-            ("cand0a", 0, CAND, 0),
-            ("cand0b", 0, CAND, HALF),
-            ("cand1a", 1, CAND, 0),
-            ("cand1b", 1, CAND, HALF),
-            ("cand0a", 1, GATE, HALF),
+        for name, b, i, lo, hi in (
+            ("gate0a", 0, GATE, 0, QUARTER),
+            ("gate0b", 0, GATE, QUARTER, HALF),
+            ("gate1a", 1, GATE, 0, HALF),
+            ("gate0c", 0, GATE, HALF, S),
+            ("cand0a", 0, CAND, 0, HALF),
+            ("cand0b", 0, CAND, HALF, S),
+            ("cand1a", 1, CAND, 0, HALF),
+            ("cand1b", 1, CAND, HALF, S),
+            ("cand0a", 1, GATE, HALF, S),
         ):
-            acc = psum.tile([P, HALF], F32, name=name)
-            product(b, i, lo, lo + HALF, acc[:])
-            activate(b, i, lo, lo + HALF, acc[:])
+            acc = psum.tile([P, hi - lo], F32, name=name)
+            product(b, i, lo, hi, acc[:])
+            activate(b, i, lo, hi, acc[:])
 
         nc.scalar.activation(old1[:], window[1][:].indirect(entries(slot_sb, S - QUARTER, S)), ACT.Copy)
         nc.vector.tensor_copy(old0[:], window[0][:].indirect(entries(slot_sb, HALF, S)))
-        old_part(0, 0, HALF)
+        old_part(0, 0, QUARTER)
+        old_part(0, QUARTER, HALF)
         nc.vector.tensor_tensor(kept[0][:, HALF:S], old0[:], keep_gate[0][:, HALF:S], ALU.mult)
         new_part(0, 0, HALF)
         new_part(0, HALF, S)

@@ -21,8 +21,8 @@ LIST_ROWS = 16
 CAND, GATE = 0, 1
 HALF = S // 2
 QUARTER = S // 4
-SPLIT = (256, 320)
-MID = 416
+SPLIT = 288
+MID = 384
 
 
 def tile_picked_gmem_tanh_e_kernel(
@@ -71,14 +71,14 @@ def tile_picked_gmem_tanh_e_kernel(
         nc.scalar.activation(warm[:, 1:2], warm[:, 0:1], ACT.Sigmoid)
 
         grouped = keep.tile([P, S, PACK], BF16, name="grouped", align_bytes=64)
-        picked = [keep.tile([P, 2, S - SPLIT[u]], BF16, name="picked%d" % u) for u in range(2)]
+        picked = [keep.tile([P, 2, S - SPLIT], BF16, name="picked%d" % u) for u in range(2)]
         x_codes = keep.tile([P, S], U32, name="x_codes", align_bytes=64)
         x_bytes = keep.tile([P, S], U8, name="x_bytes", align_bytes=64)
 
         def pair(u, lo, hi):
             nc.scalar.copy(
                 grouped[:, lo:hi, 2 * u : 2 * u + 2],
-                picked[u][:, :, lo - SPLIT[u] : hi - SPLIT[u]].rearrange("p t s -> p s t"),
+                picked[u][:, :, lo - SPLIT : hi - SPLIT].rearrange("p t s -> p s t"),
             )
 
         def quantise(lo, hi):
@@ -90,23 +90,21 @@ def tile_picked_gmem_tanh_e_kernel(
 
         for j in range(PACK):
             u = j // 2
-            split = SPLIT[u]
-            pieces = ((0, QUARTER), (QUARTER, split)) if j == PACK - 1 else ((0, split),)
+            pieces = ((0, QUARTER), (QUARTER, SPLIT)) if j == PACK - 1 else ((0, SPLIT),)
             for lo, hi in pieces:
                 nc.vector.tensor_copy(grouped[:, lo:hi, j], x_rows[j][:].indirect(entries(offs_sb, lo, hi)))
-            pieces = ((split, MID), (MID, S)) if j == PACK - 1 else ((split, S),)
+            pieces = ((SPLIT, MID), (MID, S)) if j == PACK - 1 else ((SPLIT, S),)
             for lo, hi in pieces:
                 nc.scalar.activation(
-                    picked[u][:, j % 2, lo - split : hi - split],
+                    picked[u][:, j % 2, lo - SPLIT : hi - SPLIT],
                     x_rows[j][:].indirect(entries(offs_sb, lo, hi)),
                     ACT.Copy,
                 )
             if j % 2 == 1:
                 for lo, hi in pieces:
                     pair(u, lo, hi)
-        quantise(0, QUARTER)
-        quantise(QUARTER, HALF)
-        quantise(HALF, S)
+        for lo in range(0, S, QUARTER):
+            quantise(lo, lo + QUARTER)
 
         keep_gate = [keep.tile([P, S], F32, name="keep_gate%d" % b) for b in range(2)]
         neg_cand = [keep.tile([P, S], F32, name="neg_cand%d" % b) for b in range(2)]
@@ -150,19 +148,20 @@ def tile_picked_gmem_tanh_e_kernel(
         def put0(src, lo):
             nc.scalar.activation(window[0][:].indirect(entries(slot_sb, lo, lo + HALF)), src, ACT.Copy)
 
-        for name, b, i, lo, hi in (
-            ("gate0a", 0, GATE, 0, QUARTER),
-            ("gate0b", 0, GATE, QUARTER, HALF),
-            ("gate1a", 1, GATE, 0, HALF),
-            ("gate0c", 0, GATE, HALF, S),
-            ("cand0a", 0, CAND, 0, HALF),
-            ("cand0b", 0, CAND, HALF, S),
-            ("cand1a", 1, CAND, 0, HALF),
-            ("cand1b", 1, CAND, HALF, S),
-            ("cand0a", 1, GATE, HALF, S),
+        for name, b, i, lo, hi, width in (
+            ("gate0a", 0, GATE, 0, QUARTER, QUARTER),
+            ("gate0b", 0, GATE, QUARTER, HALF, QUARTER),
+            ("gate1a", 1, GATE, 0, HALF, HALF),
+            ("gate0c", 0, GATE, HALF, S, QUARTER),
+            ("cand0a", 0, CAND, 0, HALF, HALF),
+            ("cand0b", 0, CAND, HALF, S, HALF),
+            ("cand1a", 1, CAND, 0, HALF, HALF),
+            ("cand1b", 1, CAND, HALF, S, HALF),
+            ("cand0a", 1, GATE, HALF, S, HALF),
         ):
             acc = psum.tile([P, hi - lo], F32, name=name)
-            product(b, i, lo, hi, acc[:])
+            for at in range(lo, hi, width):
+                product(b, i, at, at + width, acc[:, at - lo : at - lo + width])
             activate(b, i, lo, hi, acc[:])
 
         nc.scalar.activation(old1[:], window[1][:].indirect(entries(slot_sb, S - QUARTER, S)), ACT.Copy)

from contextlib import ExitStack

import concourse.mybir as mybir

K, T, S, N, U = 512, 1024, 512, 256, 1024
FLOPS = 2 * 2 * K * N * S

F32 = mybir.dt.float32
BF16 = mybir.dt.bfloat16
I32 = mybir.dt.int32
U32 = mybir.dt.uint32
U16 = mybir.dt.uint16
U8 = mybir.dt.uint8
FP8X4 = mybir.dt.float8_e4m3fn_x4
ACT = mybir.ActivationFunctionType
ALU = mybir.AluOpType

P = 128
PACK = 4
LIST_ROWS = 16
CAND, GATE = 0, 1
HALF = S // 2
QUARTER = S // 4
SPLIT = 288
MID = 384


def tile_picked_gmem_tanh_e_kernel(
    tc, xT, mem, w1_words, w1_scales, w2_words, w2_scales, offs, slot, out
):
    nc = tc.nc
    with ExitStack() as ctx:
        keep = ctx.enter_context(tc.tile_pool(name="keep", bufs=1))
        psum = ctx.enter_context(tc.psum_pool(name="psum", bufs=1))

        offs_sb = keep.tile([P, S // LIST_ROWS], U16, name="offs_sb")
        slot_sb = keep.tile([P, S // LIST_ROWS], U16, name="slot_sb")
        x_rows = [keep.tile([P, T], F32, name="x_row%d" % j, align_bytes=64) for j in range(PACK)]
        window = [keep.tile([P, U], F32, name="window%d" % b) for b in range(2)]
        w_codes = [keep.tile([P, N], U32, name="w_codes%d" % i, align_bytes=64) for i in range(2)]
        w_bytes = [keep.tile([P, N], U8, name="w_bytes%d" % i, align_bytes=64) for i in range(2)]
        warm = keep.tile([P, 2], F32, name="warm")

        def entries(lst, lo, hi):
            return lst[:, lo // LIST_ROWS : hi // LIST_ROWS]

        nc.vector.memset(warm[:, 0:1], 0.0)

        x_view = xT.rearrange("(p j) t -> p j t", j=PACK)

        def load_words(i, words):
            nc.sync.dma_start(w_codes[i][:].bitcast(I32), words[0].rearrange("p n t -> p (n t)").bitcast(I32))

        def load_scales(queue, i, scales):
            for q in range(4):
                queue.dma_start(
                    w_bytes[i][32 * q : 32 * q + 4, :].bitcast(I32), scales[0, 4 * q : 4 * q + 4, :].bitcast(I32)
                )

        nc.sync.dma_start(x_rows[0][:], x_view[:, 0, :])
        nc.sync.dma_start(offs_sb[:], offs)
        for j in range(1, PACK):
            nc.sync.dma_start(x_rows[j][:], x_view[:, j, :])
        nc.sync.dma_start(slot_sb[:], slot)
        load_words(GATE, w2_words)
        nc.sync.dma_start(window[0][:], mem[0:P, :])
        load_scales(nc.sync, CAND, w1_scales)
        load_words(CAND, w1_words)
        nc.sync.dma_start(window[1][:], mem[P : 2 * P, :])
        load_scales(nc.scalar, GATE, w2_scales)
        nc.scalar.activation(warm[:, 1:2], warm[:, 0:1], ACT.Sigmoid)

        grouped = keep.tile([P, S, PACK], BF16, name="grouped", align_bytes=64)
        picked = [keep.tile([P, 2, S - SPLIT], BF16, name="picked%d" % u) for u in range(2)]
        x_codes = keep.tile([P, S], U32, name="x_codes", align_bytes=64)
        x_bytes = keep.tile([P, S], U8, name="x_bytes", align_bytes=64)

        def pair(u, lo, hi):
            nc.scalar.copy(
                grouped[:, lo:hi, 2 * u : 2 * u + 2],
                picked[u][:, :, lo - SPLIT : hi - SPLIT].rearrange("p t s -> p s t"),
            )

        def quantise(lo, hi):
            nc.vector.quantize_mx(
                out=x_codes[:, lo:hi].bitcast(FP8X4),
                scales=x_bytes[:, lo:hi],
                in_=grouped[:, lo:hi, :].rearrange("p c t -> p (c t)"),
            )

        for j in range(PACK):
            u = j // 2
            pieces = ((0, QUARTER), (QUARTER, SPLIT)) if j == PACK - 1 else ((0, SPLIT),)
            for lo, hi in pieces:
                nc.vector.tensor_copy(grouped[:, lo:hi, j], x_rows[j][:].indirect(entries(offs_sb, lo, hi)))
            pieces = ((SPLIT, MID), (MID, S)) if j == PACK - 1 else ((SPLIT, S),)
            for lo, hi in pieces:
                nc.scalar.activation(
                    picked[u][:, j % 2, lo - SPLIT : hi - SPLIT],
                    x_rows[j][:].indirect(entries(offs_sb, lo, hi)),
                    ACT.Copy,
                )
            if j % 2 == 1:
                for lo, hi in pieces:
                    pair(u, lo, hi)
        for lo in range(0, S, QUARTER):
            quantise(lo, lo + QUARTER)

        keep_gate = [keep.tile([P, S], F32, name="keep_gate%d" % b) for b in range(2)]
        neg_cand = [keep.tile([P, S], F32, name="neg_cand%d" % b) for b in range(2)]
        kept = [keep.tile([P, S], F32, name="kept%d" % b) for b in range(2)]
        added = [keep.tile([P, S], F32, name="added%d" % b) for b in range(2)]
        new0 = keep.tile([P, HALF], F32, name="new0")
        old0 = keep.tile([P, HALF], F32, name="old0")
        old1 = keep.tile([P, QUARTER], F32, name="old1")

        def product(b, i, lo, hi, acc):
            nc.tensor.matmul_mx(
                out=acc,
                lhsT=w_codes[i][:, b * P : (b + 1) * P].bitcast(FP8X4),
                lhsT_scale=w_bytes[i][:, b * P : (b + 1) * P],
                rhs=x_codes[:, lo:hi].bitcast(FP8X4),
                rhs_scale=x_bytes[:, lo:hi],
                start=True,
                stop=True,
            )

        def activate(b, i, lo, hi, acc):
            if i == GATE:
                nc.scalar.activation(keep_gate[b][:, lo:hi], acc, ACT.Sigmoid, scale=-1.0)
            else:
                nc.scalar.activation(neg_cand[b][:, lo:hi], acc, ACT.Tanh, scale=-1.0)


        def old_part(b, lo, hi):
            nc.vector.tensor_tensor(
                kept[b][:, lo:hi], window[b][:].indirect(entries(slot_sb, lo, hi)), keep_gate[b][:, lo:hi], ALU.mult
            )

        def new_part(b, lo, hi):
            nc.vector.scalar_tensor_tensor(
                added[b][:, lo:hi], keep_gate[b][:, lo:hi], 1.0, neg_cand[b][:, lo:hi], ALU.subtract, ALU.mult
            )

        def join0(dst, lo):
            nc.vector.tensor_tensor(dst, kept[0][:, lo : lo + HALF], added[0][:, lo : lo + HALF], ALU.add)

        def put0(src, lo):
            nc.scalar.activation(window[0][:].indirect(entries(slot_sb, lo, lo + HALF)), src, ACT.Copy)

        for name, b, i, lo, hi, width in (
            ("gate0a", 0, GATE, 0, QUARTER, QUARTER),
            ("gate0b", 0, GATE, QUARTER, HALF, QUARTER),
            ("gate1a", 1, GATE, 0, HALF, HALF),
            ("gate0c", 0, GATE, HALF, S, QUARTER),
            ("cand0a", 0, CAND, 0, HALF, HALF),
            ("cand0b", 0, CAND, HALF, S, HALF),
            ("cand1a", 1, CAND, 0, HALF, HALF),
            ("cand1b", 1, CAND, HALF, S, HALF),
            ("cand0a", 1, GATE, HALF, S, HALF),
        ):
            acc = psum.tile([P, hi - lo], F32, name=name)
            for at in range(lo, hi, width):
                product(b, i, at, at + width, acc[:, at - lo : at - lo + width])
            activate(b, i, lo, hi, acc[:])

        nc.scalar.activation(old1[:], window[1][:].indirect(entries(slot_sb, S - QUARTER, S)), ACT.Copy)
        nc.vector.tensor_copy(old0[:], window[0][:].indirect(entries(slot_sb, HALF, S)))
        old_part(0, 0, QUARTER)
        old_part(0, QUARTER, HALF)
        nc.vector.tensor_tensor(kept[0][:, HALF:S], old0[:], keep_gate[0][:, HALF:S], ALU.mult)
        new_part(0, 0, HALF)
        new_part(0, HALF, S)
        join0(new0[:], 0)
        put0(new0[:], 0)
        old_part(1, 0, HALF)
        new_part(1, 0, S)
        old_part(1, HALF, S - QUARTER)
        nc.vector.tensor_tensor(kept[1][:, S - QUARTER : S], old1[:], keep_gate[1][:, S - QUARTER : S], ALU.mult)
        join0(keep_gate[1][:, 0:HALF], HALF)
        put0(keep_gate[1][:, 0:HALF], HALF)
        nc.sync.dma_start(out[0:P, :], window[0][:])
        nc.vector.tensor_tensor(window[1][:].indirect(slot_sb[:]), kept[1][:], added[1][:], ALU.add)
        nc.sync.dma_start(out[P : 2 * P, :], window[1][:])
